import numpy as np, ml_dtypes
CORES = [24,25,26,27,28,29,30,31]
N = 8
BF = ml_dtypes.bfloat16
L, M, P, RO = 256, 2048, 1, 4
PLANT = [[197, 0, 2], [1155, 1, 8], [196, 0, 0]]
LIMS = [[0, 2], [4, 12]]
BRINK = 1592
def skew(rng):
    return np.minimum((M * rng.random((N, 8, 16, L)) ** rng.choice(np.array([0.5, 1.0, 2.0]), (N, 8, 16, 1))).astype(np.int64), M - 1)
def parts(rng):
    col = skew(rng); om = np.where(rng.random((N, 8, 16, L)) < rng.choice(np.array([0.4, 0.7, 0.95]), (N, 8, 1, 1)), skew(rng), 0)
    who = np.minimum((16 * rng.random((N, 8, L)) ** rng.choice(np.array([1.5, 2.0, 3.0]), (1, 8, 1))).astype(np.int64), 15)
    order = np.argsort(rng.random((8, 16)), axis=1); mem = order[np.arange(8)[None, :, None], who]
    th = np.minimum(np.maximum(rng.permutation(np.array([1, 2, 3, 4, 6, 8, 9, 11]))[None, :] + rng.integers(-1, 2, (N, 8)), 1), 16)
    return col, om, mem, th
def pack(col, om, mem, th):
    return {"col": np.ascontiguousarray(col.reshape(N, 128, L)).astype(np.int32), "om": np.ascontiguousarray(om.reshape(N, 128, L)).astype(np.int32),
            "mem": np.ascontiguousarray(mem).astype(np.int32), "th": np.ascontiguousarray(th.reshape(N, 8, 1)).astype(np.int32)}
def near(rng, g, col, om, mem, th):
    s = int(rng.integers(0, N)); b = rng.permutation(16)
    col[:, g] = np.maximum(skew(rng)[:, g], 1); om[:, g] = 0; mem[:, g] = b[rng.integers(3, 16, (N, L))]
    for n, k, c in PLANT:
        r, i = (n // L + s) % N, n % L
        mem[r, g, i] = b[k]; om[r, g, b[(k + np.arange(c)) % 16], i] = 1
    for r, v in LIMS: th[(r + s) % N, g] = v
def brink(rng, g, col, om, mem, th):
    b = rng.permutation(16); r, i = BRINK // L, BRINK % L; v = rng.integers(1, M - 1, 2)
    col[:, g] = np.minimum(col[:, g], M - 2); col[:, g, b[2:4]] = 0; col[N - 1, g, b[2:4], L - 1] = v
    om[:, g] = 0; om[r, g, b[2:4], i] = rng.integers(1, v + 1)
    mem[:, g] = b[0]; mem[r, g, i] = b[1]; th[r, g] = 2
def setup_inputs(rng):
    return pack(*parts(rng))
def setup_inputs_lone(rng):
    col, om, mem, th = parts(rng)
    for g in (0, 2, 4, 6): mem[:, g] = rng.integers(0, 16)
    for g in (1, 5): mem[:, g] = ((np.arange(N) + rng.integers(0, 16)) & 15)[:, None]
    a, b = rng.permutation(16)[:2]
    mem[:, 3] = np.where(mem[:, 3] == a, b, mem[:, 3]); mem[N - 1, 3, L - 1] = a
    mem[:, 7] = np.where(mem[:, 7] == b, a, mem[:, 7]); mem[0, 7, 0] = b
    return pack(col, om, mem, th)
def setup_inputs_ties(rng):
    col, om, mem, th = parts(rng)
    v = rng.integers(1, M - 1, (8, 6)); v[:, 0] = 0; v[:, 1] = M - 1; g = np.arange(8)[None, :, None, None]
    col = v[g, rng.integers(0, 6, (N, 8, 16, L))]; om = v[g, rng.integers(0, 6, (N, 8, 16, L))]
    near(rng, int(rng.integers(0, 8)), col, om, mem, th)
    return pack(col, om, mem, th)
def setup_inputs_ends(rng):
    col, om, mem, th = parts(rng); q = rng.permutation(8); th = rng.integers(1, 17, (N, 8))
    col[:, q[:3]] = np.maximum(col[:, q[:3]], 1); om[:, q[:3]] = 1
    om[:, q[1], rng.integers(0, 16)] = 0; om[:, q[2], rng.integers(0, 16)] = 0
    th[:, q[0]] = 16; th[:, q[1]] = 16; th[:, q[2]] = 15; th[rng.integers(0, N), q[1]] = 1
    om[:, q[3]] = 0; th[:, q[3]] = 1; om[:, q[4]] = M - 1; col[:, q[4], ::3] = M - 1; th[:, q[4]] = rng.integers(1, 4, N); th[:, q[5]] = 1
    k, j = rng.permutation(16)[:2]; v = int(rng.integers(1, M - 1))
    c = np.maximum(col[:, q[6]], 1); c = np.where(c == v, v + 1, c); c[:, k] = v; c[v // L, j, v % L] = 0
    col[:, q[6]] = c; om[:, q[6]] = 1; th[:, q[6]] = 16
    brink(rng, int(q[7]), col, om, mem, th)
    return pack(col, om, mem, th)
def setup_inputs_far(rng):
    col, om, mem, th = parts(rng)
    col[:, ::2] = ((np.arange(N) + 1) % N * L)[:, None, None, None] + rng.integers(0, L, (N, 4, 16, L))
    col[:, 1] = rng.integers(0, 16, (N, 16, L)); col[:, 5] = rng.integers(0, 16, (N, 16, L))
    for g in (0, 1, 4, 5): mem[:, g] = rng.permutation(16)[:2][rng.integers(0, 2, (N, L))]
    return pack(col, om, mem, th)
def setup_inputs_spread(rng):
    col, om, mem, th = parts(rng); h = np.log2(M)
    col = np.minimum((np.exp2(h * rng.random((N, 8, 1, L)) ** 0.5) * rng.random((N, 8, 16, L))).astype(np.int64), M - 1)
    om = np.minimum((np.exp2(h * rng.random((N, 8, 16, L))) - 1).astype(np.int64), M - 1)
    th = np.minimum(np.exp2(4.1 * rng.random((N, 8))).astype(np.int64), 16); th[:, rng.integers(0, 8)] = 1
    return pack(col, om, mem, th)
def check_inputs(d):
    bad = []
    for k, lo, hi in (("col", 0, M - 1), ("om", 0, M - 1), ("mem", 0, 15), ("th", 1, 16)):
        if np.min(d[k]) < lo or np.max(d[k]) > hi: bad.append("range of " + k)
    return bad
def reference(col, om, mem, th):
    def joined(a): return np.ascontiguousarray(a.astype(np.int64).reshape(N, 8, 16, L).transpose(1, 2, 0, 3)).reshape(8, 16, M)
    def parted(a): return np.ascontiguousarray(a.reshape(8, 16, N, L).transpose(2, 0, 1, 3)).reshape(N, 128, L)
    vec = np.zeros((8, 16, M * (RO + 1)), np.int64); vec[:, :, :M] = joined(col)
    w = joined(om); R = np.zeros((8, M), np.int64); S = np.zeros((8, M), np.int64)
    one = mem.astype(np.int64).transpose(1, 0, 2).reshape(8, 1, M) == np.arange(16)[None, :, None]
    lim = np.repeat(th.astype(np.int64)[:, :, 0].T, L, axis=1); lane = np.arange(M); i = np.tile(np.arange(L), N); none = 2 ** 20
    hist = []
    for t in range(RO):
        last = vec[:, :, M * t:M * (t + 1)]; e = M * (t + 1) + lane
        par = [(last, w, R)]
        for p in range(P):
            o = (5 * i + (lane - i) + 61 * S + 16 * R + 77 * t + 341 * p) & (M - 1)
            par.append((np.take_along_axis(last, o[:, None, :], 2), np.take_along_axis(w, o[:, None, :], 2), np.take_along_axis(R, o, 1)))
        x = np.where(one, e, np.maximum.reduce([a[0] for a in par]))
        vec[:, :, M * (t + 1):M * (t + 2)] = x
        top = np.maximum.reduce([a[2] for a in par])
        low = np.minimum.reduce([np.where((a[2] == top)[:, None, :] & (a[1] > 0), a[1], none) for a in par])
        c = np.zeros((8, 16, M), np.int64)
        for k in range(16):
            c += np.take_along_axis(vec, x[:, k:k + 1, :], 2) >= low
        S = np.add.reduce((c >= lim[:, None, :]).astype(np.int64), axis=1)
        up = S >= lim; R = top + up
        w = np.where(up[:, None, :], np.where(one, e, 0), np.where(low == none, 0, low))
        hist.append(R)
    yr = np.ascontiguousarray(np.stack(hist).reshape(RO, 8, N, L).transpose(2, 1, 0, 3)).reshape(N, 8, RO * L)
    return {"yx": parted(x).astype(np.float32), "yo": parted(w).astype(np.float32), "yr": yr.astype(np.float32)}

@@ -1,0 +1,312 @@
+from concourse.bass import DstId, RemoteDMATransfer
+from concourse.mybir import AluOpType, ActivationFunctionType
+
+L, M, RO = 256, 2048, 4
+H = L // 2
+K = 16384.0
+BIG = 65536.0
+FR = 1024
+SPLIT = [32, 96, 96, 96]
+HALVES = [True, False, False, False]
+
+SCRATCH = {"p%d" % b: ("psum", [128, 512], "float32") for b in range(8)}
+for dtype, tiles in (
+        ("float32", dict(tab=FR + 4 * M, wt=3 * M, gat=16 * L, cols=8, base=64, one=L, m1=L, m2=L, xs=L, ks=L, ua=48,
+                         tmp=L, kn=L, ox=L, oo=L)),
+        ("bfloat16", dict(cmp=16 * L, ones=144, ident=128, bo=128, zs=144, zt=144, et=24, u1=L, bb=L, sb=L)),
+        ("int32", dict(coli=L, omi=L, pi=8, zi=L, ui=32, key=L, qi=L)),
+        ("uint16", dict(off=L, ol=16))):
+    SCRATCH.update({name: ("sbuf", [128, n], dtype) for name, n in tiles.items()})
+SCRATCH.update({"mti": ("sbuf", [8, 264], "int32"), "mtb": ("sbuf", [8, 264], "bfloat16"),
+                "e1": ("sbuf", [8, 128], "bfloat16"), "ey": ("sbuf", [8, 272], "bfloat16"),
+                "orr": ("sbuf", [8, RO * L], "float32")})
+SEMAPHORES = (["qv", "qa", "qt", "qg", "sent"] + ["arr%d" % k for k in range(12)] + ["dma%d" % k for k in range(14)])
+
+A = AluOpType
+F = ActivationFunctionType
+
+
+def rank_program(g, core, T, topo):
+    r = T.rank_of(core)
+    if r is None:
+        return
+    others = [c for c in T.cores if c != core]
+    queue = {"v": g.vector, "a": g.scalar, "t": g.tensor, "g": g, "s": g.sync}
+    own = {"v": "qv", "a": "qa", "t": "qt", "g": "qg"}
+    total, seen, wrote, read, bank = {}, {}, {}, {}, {}
+    count = {"dma": 0, "arr": 0}
+
+    def wait(q, tok):
+        if seen.get((q, tok[0]), 0) < tok[1]:
+            queue[q].wait_ge(T.sem[tok[0]], tok[1])
+            seen[(q, tok[0])] = tok[1]
+
+    def order(q, rd, wr, banks):
+        need = {}
+        toks = [wrote[k] for k in rd + wr if k in wrote] + [t for k in wr for t in read.get(k, [])]
+        toks += [t for b in banks for e, t in bank.get(b, {}).items() if e != q]
+        for s, n in toks:
+            if not (q == "t" and s == "qt"):
+                need[s] = max(need.get(s, 0), n)
+        for s in need:
+            wait(q, (s, need[s]))
+
+    def note(q, tok, rd, wr, banks):
+        for k in rd:
+            read.setdefault(k, []).append(tok)
+        for k in wr:
+            wrote[k] = tok
+            read[k] = []
+        for b in banks:
+            bank.setdefault(b, {})[q] = tok
+
+    def op(q, call, rd, wr, banks=(), inc=True):
+        order(q, rd, wr, banks)
+        ins = call()
+        n = total.get(own[q], 0) + 1
+        if inc:
+            ins.then_inc(T.sem[own[q]], 1)
+            total[own[q]] = n
+        note(q, (own[q], n), rd, wr, banks)
+
+    def dma(q, out, in_, rd, wr):
+        order(q, rd, wr, ())
+        s = "dma%d" % count["dma"]
+        count["dma"] += 1
+        queue[q].dma_start(out, in_).then_inc(T.sem[s], 16)
+        total[s] = 16
+        note(q, (s, 16), rd, wr, ())
+
+    def spread(src, dst, rd, key):
+        order("g", rd, [], ())
+        s = "arr%d" % count["arr"]
+        count["arr"] += 1
+        mask = topo.mask(core, others[0])
+        for c in others:
+            mask &= topo.mask(core, c)
+        n = bin(mask).count("1")
+        ids = [DstId(rid=topo.addr(c)[0], pnc=topo.addr(c)[1]) for c in others]
+        g.remote_dma_fused([RemoteDMATransfer(dst_ids=ids, dma_engine_mask=mask, remote_sem=T.sem[s],
+                                              srcs=[src], dsts=[dst] * len(others))], local_sem=T.sem.sent)
+        total["sent"] = total.get("sent", 0) + n
+        total[s] = n * len(others)
+        wrote[key] = (s, total[s])
+
+    V, S, P = g.vector, g.scalar, g.tensor
+
+    def ts(out, in0, s1, s2, o0, o1, rd, wr, banks=()):
+        if o1 is None:
+            op("v", lambda: V.tensor_scalar(out, in0, s1, None, o0), rd, wr, banks)
+        else:
+            op("v", lambda: V.tensor_scalar(out, in0, s1, s2, o0, o1), rd, wr, banks)
+
+    def tt(out, in0, in1, o, rd, wr, banks=()):
+        op("v", lambda: V.tensor_tensor(out, in0, in1, o), rd, wr, banks)
+
+    def cp(out, in_, rd, wr, banks=()):
+        op("v", lambda: V.tensor_copy(out, in_), rd, wr, banks)
+
+    def act(out, in_, f, bias, scale, rd, wr, banks=()):
+        op("a", lambda: S.activation(out, in_, f, bias=bias, scale=scale), rd, wr, banks)
+
+    def mm(out, lhsT, rhs, start, stop, rd, wr, banks, inc=True):
+        op("t", lambda: P.matmul(out, lhsT, rhs, start, stop), rd, wr, banks, inc)
+
+    def sec(s):
+        return FR + M * s
+
+    def both(k):
+        return [k + "0", k + "1"]
+
+    lo, mp = T.p0[:, 0:L], T.p0[:, L:2 * L]
+    dd, ee = T.p6[:, 0:L], T.p7[:, 0:L]
+    thc, bc, jc = T.cols[:, 0:1], T.cols[:, 1:2], T.cols[:, 2:3]
+
+    def make_dd(t):
+        act(dd, T.one[:], F.Identity, L * (t + 1) - 0.25, -float(M * (t + 1) + L * r + L * (t + 1)), ["one"], ["dd"], [6])
+
+    def make_ee(t):
+        act(ee, T.m1[:], F.Relu, M * (t + 1) - BIG, 1.0, ["m1"], ["ee"], [7])
+
+    def make_cc(t):
+        act([T.p6, T.p7][t % 2][:, L:2 * L], T.m2[:], F.Relu, K - M * (t + 1) - BIG, 1.0, ["m2"], ["cc%d" % (t % 2)], [6 + t % 2])
+
+    def lanes_down(out, lhs, rhs, rd, wr, b):
+        for p in range(16):
+            mm(out, lhs[:, 15 - p:143 - p], rhs[:, p:L:16], p == 0, p == 15, rd, wr, [b], p == 15)
+
+    dma("s", T.coli[:], T.col[:], [], ["col"])
+    dma("a", T.omi[:], T.om[:], [], ["om"])
+    dma("s", T.mti[:, 0:L], T.mem[:], [], ["mem"])
+    dma("a", T.mti[:, L:L + 1], T.th[:], [], ["th"])
+    op("v", lambda: V.memset(T.ones[:], 1.0), [], ["ones"])
+    op("v", lambda: V.memset(T.u1[:], K), [], both("u1"))
+    op("g", lambda: g.iota(T.pi[:, 0:1], [[0, 1]], 0, 1), [], ["pi"])
+    op("g", lambda: g.iota(T.base[:], [[77, 4], [80, 16]], L * r, 0, allow_small_or_imprecise_dtypes=True), [], ["base"])
+    op("g", lambda: g.affine_select(T.e1[:], T.ones[0:8, 0:128], [[1, 128]], A.is_ge, 0.0, 0, -16), ["ones"], ["e1"])
+    op("g", lambda: g.affine_select(T.ey[:, 128:272], T.ones[0:8, :], [[1, 144]], A.is_equal, 0.0, -15, -16), ["ones"], ["ey1"])
+    op("g", lambda: g.affine_select(T.ey[:, 0:128], T.e1[:], [[-1, 128]], A.is_ge, 0.0, 15, 16), ["e1"], ["ey0"])
+    mine = T.tab[:, sec(0) + L * r:sec(0) + L * (r + 1)]
+    ts(mp, T.omi[:], 1.0 / 8192, None, A.mult, None, ["om"], both("mp"), [0])
+    tt(mine, T.coli[:], mp, A.add, ["col"] + both("mp"), ["own0"], [0])
+    spread(mine, mine, ["own0"], "far0")
+
+    op("g", lambda: g.iota(T.m1[:], [[1, L]], int(BIG) + L * r, 0, allow_small_or_imprecise_dtypes=True), [], ["m1"])
+    op("g", lambda: g.affine_select(T.ident[:], T.ones[:, 0:128], [[-1, 128]], A.is_equal, 0.0, 0, 1), ["ones"], ["ident"])
+    ts(T.pi[:, 4:5], T.pi[:, 0:1], 15, None, A.bitwise_and, None, ["pi"], ["pj"])
+    cp(jc, T.pi[:, 4:5], ["pj"], ["jc"])
+    ts(T.cols[:, 3:4], T.pi[:, 4:5], 5.0, None, A.mult, None, ["pj"], ["j5"])
+    cp(T.mtb[:, 0:L + 1], T.mti[:, 0:L + 1], ["mem", "th"], ["mtb"])
+    mm(T.p1[:, 0:272], T.ey[:, 0:128], T.ey[:], True, True, ["ey0", "ey1"], ["c1"], [1])
+    mm(T.p2[:, 0:L + 1], T.ey[:, 0:128], T.mtb[:, 0:L + 1], True, True, ["ey0", "mtb"], ["c2"], [2])
+    ts(T.ui[:, 0:16], T.base[:, 0:16], T.cols[:, 3:4], None, A.add, None, ["base", "j5"], ["u4"])
+    ts(T.ui[:, 16:32], T.ui[:, 0:16], M - 1, None, A.bitwise_and, None, ["u4"], ["u5"])
+    cp(T.ol[:], T.ui[:, 16:32], ["u5"], ["ol"])
+    ts(T.one[:], T.p2[:, 0:L], jc, None, A.is_equal, None, ["c2", "jc"], ["one"], [2])
+    cp(thc, T.p2[:, L:L + 1], ["c2"], ["thc"], [2])
+    ts(T.m2[:], T.m1[:], -1.0, 2 * BIG, A.mult, A.add, ["m1"], ["m2"])
+    tt(T.m1[:], T.m1[:], T.one[:], A.mult, ["m1", "one"], ["m1"])
+    make_dd(0)
+    make_ee(0)
+    tt(T.m2[:], T.m2[:], T.one[:], A.mult, ["m2", "one"], ["m2"])
+    tt(T.xs[:], mine, ee, A.max, ["own0", "ee"], ["xs"], [7])
+    make_cc(0)
+    make_ee(1)
+    ts(T.zi[:], T.omi[:], -1.0, None, A.mult, None, ["om"], both("zi"))
+    ts(T.qi[:], T.zi[:], 4095, None, A.bitwise_and, None, both("zi"), ["qi"])
+    cp(mp, T.qi[:], ["qi"], both("mp"), [0])
+    ts(T.bo[:], T.p1[:, 0:128], 131072.0, None, A.mult, None, ["c1"], ["bo"], [1])
+    ts(T.zs[:], T.p1[:, 128:272], 61.0, None, A.mult, None, ["c1"], ["zs"], [1])
+    ts(T.zt[:], T.p1[:, 128:272], 1.0 / K, None, A.mult, None, ["c1"], ["zt"], [1])
+    for n, wgt in enumerate([1.0 / (16 * K), 1.0 / 32, 1.0 / 16]):
+        ts(T.et[:, 8 * n:8 * n + 8], T.p1[:, 0:128:16], wgt, None, A.mult, None, ["c1"], ["et%d" % n], [1])
+    ts(bc, thc, -1.0 / 16, 1.0 / 32, A.mult, A.add, ["thc"], ["bc"])
+    ts(T.cols[:, 4:5], thc, 61.0, -46.5, A.mult, A.add, ["thc"], ["c4"])
+    ts(T.base[:], T.base[:], T.cols[:, 3:4], T.cols[:, 4:5], A.add, A.add, ["base", "j5", "c4"], ["base"])
+    lanes_down(T.p5[:, 0:16], T.zt, T.u1, ["zt"] + both("u1"), ["tl"], 5)
+
+    for t in range(RO):
+        last = t == RO - 1
+        f0 = FR - L * (t + 1)
+        a = SPLIT[t]
+        par = T.tab[:, sec(t):sec(t + 1)]
+        tabs = ["own%d" % s for s in range(t + 1)] + ["far%d" % s for s in range(t + 1)]
+        fs = both("f%d_" % t)
+        for h in (1, 0):
+            i0, i1 = H * h, H * h + H
+            tt(T.tab[:, f0 + i0:f0 + i1], par.indirect(T.ol[:, i0 // 16:i1 // 16]), T.xs[:, i0:i1], A.max,
+               ["own%d" % t, "far%d" % t, "ol", "xs"], [fs[h]])
+            tt(T.zi[:, i0:i1], T.tab[:, f0 + i0:f0 + i1], T.p6[:, i0:i1], A.add, [fs[h], "dd"], ["zi%d" % h], [6])
+            ts(T.off[:, i0:i1], T.zi[:, i0:i1], -float(i0), None, A.add, None, ["zi%d" % h], ["off%d" % h])
+            c0 = max(i0, a)
+            act(T.gat[:, 16 * c0:16 * i1], T.tab[:, f0 + i0:sec(t + 1)].indirect(T.off[:, c0:i1]), F.Copy, 0.0, 1.0,
+                tabs + fs[h:] + ["off%d" % h], ["ga%d" % h])
+        xnew = T.tab[:, f0:f0 + L]
+        if not last:
+            slot = T.tab[:, sec(t + 1) + L * r:sec(t + 1) + L * (r + 1)]
+            spread(xnew, slot, fs, "far%d" % (t + 1))
+            dma("s", slot, xnew, fs, ["own%d" % (t + 1)])
+        if t == 0:
+            ts(T.key[:], par.indirect(T.ol[:]), -8192.0, None, A.mult, None, ["own0", "far0", "ol"], ["key"])
+            ts(T.qi[:], T.key[:], 4095, None, A.bitwise_and, None, ["key"], ["qi"])
+            tt(T.tmp[:], T.qi[:], mp, A.max, ["qi"] + both("mp"), ["tmp"], [0])
+            ts(lo, T.tmp[:], -1.0, 4096.0, A.mult, A.add, ["tmp"], ["lo"], [0])
+            ts(mp, T.tmp[:], 0.0, 12288.0, A.is_gt, A.mult, ["tmp"], both("mp"), [0])
+            tt(T.key[:], mp, T.tmp[:], A.add, both("mp") + ["tmp"], ["key"], [0])
+            tt(T.kn[:], T.u1[:], T.p6[:, L:2 * L], A.add, both("u1") + ["cc0"], both("kn"), [6])
+        cp(T.gat[:, 0:16 * a], T.tab[:, f0:sec(t + 1)].indirect(T.off[:, 0:a]), tabs + fs + ["off0"], ["gv"])
+        if t > 0:
+            w0 = M * (t - 1)
+            cp(T.ks[:], T.wt[:, w0 + L * r:w0 + L * (r + 1)], both("wown%d_" % t), ["ks"])
+        if not last:
+            tt(T.xs[:], xnew, ee, A.max, fs + ["ee"], ["xs"], [7])
+            make_dd(t + 1)
+            if t + 2 < RO:
+                make_cc(t + 1)
+                make_ee(t + 2)
+        else:
+            ts(T.zi[:], xnew, -0.25, None, A.add, None, fs, both("zi"))
+            cp(T.ox[:], T.zi[:], both("zi"), ["ox"])
+            dma("s", T.yx[:], T.ox[:], ["ox"], [])
+        if t > 0:
+            tt(T.key[:], T.wt[:, w0:w0 + M].indirect(T.ol[:]), T.ks[:], A.max,
+               both("wown%d_" % t) + both("wfar%d_" % t) + ["ol", "ks"], ["key"])
+            ts(T.qi[:], T.key[:], int(K) - 1, None, A.bitwise_and, None, ["key"], ["qi"])
+            ts(lo, T.qi[:], -1.0, K, A.mult, A.add, ["qi"], ["lo"], [0])
+
+        def hk(k, hs):
+            return ["%s%d" % (k, h) for h in hs]
+
+        def compare(hs, k):
+            i0, i1, b = H * hs[0], H * hs[-1] + H, 1 + hs[0]
+            ck = hk("cmp%d_" % k, hs)
+            tt(T.cmp[:, L * k + i0:L * k + i1], T.gat[:, 16 * i0 + k:16 * i1:16], T.p0[:, i0:i1], A.is_ge,
+               hk("ga", hs) + (["gv"] if hs[0] == 0 else []) + ["lo"], ck, [0])
+            mm([T.p1, T.p2][hs[0]][:, i0:i1], T.ident[:], T.cmp[:, L * k + i0:L * k + i1], k == 0, k == 15,
+               ck + ["ident"], ["c%d" % b], [b], k == 15)
+
+        def counted(hs, final):
+            i0, i1, b = H * hs[0], H * hs[-1] + H, 1 + hs[0]
+            if t > 0:
+                tt(T.u1[:, i0:i1], T.key[:, i0:i1], T.p0[:, i0:i1], A.add, ["key", "lo"], hk("u1", hs), [0])
+                if final and not last:
+                    lanes_down(T.p5[:, 0:16], T.zt, T.u1, ["zt"] + both("u1"), ["tl"], 5)
+            if last:
+                ts(T.tmp[:, i0:i1], T.p0[:, i0:i1], K, None, A.is_lt, None, ["lo"], hk("tmp", hs) + ["tmp"], [0])
+            ts(T.bb[:, i0:i1], [T.p1, T.p2][hs[0]][:, i0:i1], thc, bc, A.is_ge, A.add, ["c%d" % b, "thc", "bc"], hk("bb", hs), [b])
+            mm(T.p3[:, i0:i1], T.bo[:], T.bb[:, i0:i1], True, True, hk("bb", hs) + ["bo"], hk("sj", hs), [3])
+            if final and not last:
+                lanes_down(T.p4[:, 0:16], T.zs, T.bb, both("bb") + ["zs"], ["sl"], 4)
+            if last:
+                tt(T.kn[:, i0:i1], T.tmp[:, i0:i1], T.p0[:, i0:i1], A.mult, hk("tmp", hs) + ["lo"], hk("kn", hs), [0])
+                tt(T.p0[:, L + i0:L + i1], T.p7[:, i0:i1], T.kn[:, i0:i1], A.subtract, ["ee"] + hk("kn", hs), hk("mp", hs), [0, 7])
+            elif t > 0:
+                tt(T.kn[:, i0:i1], T.u1[:, i0:i1], [T.p6, T.p7][t % 2][:, L + i0:L + i1], A.add,
+                   hk("u1", hs) + ["cc%d" % (t % 2)], hk("kn", hs), [6 + t % 2])
+
+        def risen(hs):
+            i0, i1 = H * hs[0], H * hs[-1] + H
+            m = T.p0[:, L + i0:L + i1]
+            if not last:
+                wn = T.wt[:, M * t + L * r + i0:M * t + L * r + i1]
+                tt(m, T.p3[:, i0:i1], T.kn[:, i0:i1], A.min, hk("sj", hs) + hk("kn", hs), hk("mp", hs), [0, 3])
+                tt(wn, m, T.key[:, i0:i1], A.max, hk("mp", hs) + ["key"], hk("wown%d_" % (t + 1), hs), [0])
+                spread(wn, wn, hk("wown%d_" % (t + 1), hs), "wfar%d_%d" % (t + 1, hs[0]))
+            else:
+                ts(T.sb[:, i0:i1], T.p3[:, i0:i1], 0.0, None, A.is_gt, None, hk("sj", hs), hk("sb", hs), [3])
+                tt(m, T.sb[:, i0:i1], m, A.mult, hk("sb", hs) + hk("mp", hs), hk("mp", hs), [0])
+                tt(T.oo[:, i0:i1], m, T.kn[:, i0:i1], A.add, hk("mp", hs) + hk("kn", hs), hk("oo", hs), [0])
+                dma("s", T.yo[:, i0:i1], T.oo[:, i0:i1], hk("oo", hs), [])
+
+        if HALVES[t]:
+            for k in range(16):
+                compare([1], k)
+            for k in range(16):
+                compare([0], k)
+                if k == 1:
+                    counted([1], False)
+                if k == 3:
+                    risen([1])
+            counted([0], True)
+            risen([0])
+        else:
+            for k in range(16):
+                compare([0, 1], k)
+            counted([0, 1], True)
+            risen([0, 1])
+        if not last:
+            act(T.sb[:], T.p3[:, 0:L], F.Sign, 0.0, 1.0, both("sj"), both("sb"), [3])
+            tt(T.ua[:, 0:16], T.p5[:, 0:16], T.base[:, 16 * t + 16:16 * t + 32], A.add, ["tl", "base"], ["u0"], [5])
+            ts(T.ua[:, 16:32], T.p4[:, 0:16], 0.0, 16.0, A.is_gt, A.mult, ["sl"], ["u1a"], [4])
+            tt(T.ua[:, 32:48], T.p4[:, 0:16], T.ua[:, 0:16], A.add, ["sl", "u0"], ["u2"], [4])
+            tt(T.ui[:, 0:16], T.ua[:, 16:32], T.ua[:, 32:48], A.add, ["u1a", "u2"], ["u4"])
+            ts(T.ui[:, 16:32], T.ui[:, 0:16], M - 1, None, A.bitwise_and, None, ["u4"], ["u5"])
+            cp(T.ol[:], T.ui[:, 16:32], ["u5"], ["ol"])
+        rr = T.p5[0:8, L:2 * L]
+        n = 2 if last else 1
+        mm(rr, T.et[:, 0:8], T.u1[:], True, False, ["et0"] + both("u1"), ["rr"], [5], False)
+        mm(rr, T.et[:, 8 * n:8 * n + 8], T.sb[:], False, True, ["et%d" % n] + both("sb"), ["rr"], [5])
+        act(T.orr[:, L * t:L * t + L], rr, F.Identity, -1.0 if last else -0.5, 1.0, ["rr"], ["orr"], [5])
+    dma("a", T.yr[:], T.orr[:], ["orr"], [])
+    for s in total:
+        wait("g", (s, total[s]))

@@ -2,12 +2,12 @@ from concourse.bass import DstId, RemoteDMATransfer
 from concourse.mybir import AluOpType, ActivationFunctionType
 
 L, M, RO = 256, 2048, 4
-H = L // 2
+CUT = [0, 128, L]
 K = 16384.0
 BIG = 65536.0
+WHOLE = 12582912.0
 FR = 1024
-SPLIT = [32, 96, 96, 96]
-HALVES = [True, False, False, False]
+SPLIT = [32, 100, 100, 100]
 
 SCRATCH = {"p%d" % b: ("psum", [128, 512], "float32") for b in range(8)}
 for dtype, tiles in (
@@ -20,7 +20,8 @@ for dtype, tiles in (
 SCRATCH.update({"mti": ("sbuf", [8, 264], "int32"), "mtb": ("sbuf", [8, 264], "bfloat16"),
                 "e1": ("sbuf", [8, 128], "bfloat16"), "ey": ("sbuf", [8, 272], "bfloat16"),
                 "orr": ("sbuf", [8, RO * L], "float32")})
-SEMAPHORES = (["qv", "qa", "qt", "qg", "sent"] + ["arr%d" % k for k in range(12)] + ["dma%d" % k for k in range(14)])
+SEMAPHORES = (["qv", "qa", "qt", "qg", "sent"] + ["arr%d" % k for k in range(7)] + ["via%d" % k for k in range(7)]
+              + ["dma%d" % k for k in range(7)])
 
 A = AluOpType
 F = ActivationFunctionType
@@ -30,7 +31,10 @@ def rank_program(g, core, T, topo):
     r = T.rank_of(core)
     if r is None:
         return
-    others = [c for c in T.cores if c != core]
+    here = [c for c in T.cores if topo.die(c) == topo.die(core)]
+    there = [c for c in T.cores if topo.die(c) != topo.die(core)]
+    partner = there[here.index(core)]
+    near = [c for c in here if c != core]
     queue = {"v": g.vector, "a": g.scalar, "t": g.tensor, "g": g, "s": g.sync}
     own = {"v": "qv", "a": "qa", "t": "qt", "g": "qg"}
     total, seen, wrote, read, bank = {}, {}, {}, {}, {}
@@ -43,7 +47,7 @@ def rank_program(g, core, T, topo):
 
     def order(q, rd, wr, banks):
         need = {}
-        toks = [wrote[k] for k in rd + wr if k in wrote] + [t for k in wr for t in read.get(k, [])]
+        toks = [wrote[k] for k in rd + wr + [k + "v" for k in rd] if k in wrote] + [t for k in wr for t in read.get(k, [])]
         toks += [t for b in banks for e, t in bank.get(b, {}).items() if e != q]
         for s, n in toks:
             if not (q == "t" and s == "qt"):
@@ -77,20 +81,27 @@ def rank_program(g, core, T, topo):
         total[s] = 16
         note(q, (s, 16), rd, wr, ())
 
-    def spread(src, dst, rd, key):
+    eng = [e for e in topo.engines(core, partner) if all(e in topo.engines(core, c) for c in near)]
+
+    def send(cores, sem, src, dst):
+        g.remote_dma_fused([RemoteDMATransfer(dst_ids=[DstId(rid=topo.addr(c)[0], pnc=topo.addr(c)[1]) for c in cores],
+                                              dma_engine_mask=sum(1 << e for e in eng), remote_sem=T.sem[sem],
+                                              srcs=[src], dsts=[dst] * len(cores))], local_sem=T.sem.sent)
+        total["sent"] = total.get("sent", 0) + len(eng)
+
+    def spread(src, slot, rd, key):
         order("g", rd, [], ())
-        s = "arr%d" % count["arr"]
+        s, v = "arr%d" % count["arr"], "via%d" % count["arr"]
         count["arr"] += 1
-        mask = topo.mask(core, others[0])
-        for c in others:
-            mask &= topo.mask(core, c)
-        n = bin(mask).count("1")
-        ids = [DstId(rid=topo.addr(c)[0], pnc=topo.addr(c)[1]) for c in others]
-        g.remote_dma_fused([RemoteDMATransfer(dst_ids=ids, dma_engine_mask=mask, remote_sem=T.sem[s],
-                                              srcs=[src], dsts=[dst] * len(others))], local_sem=T.sem.sent)
-        total["sent"] = total.get("sent", 0) + n
-        total[s] = n * len(others)
+        send([partner], v, src, slot(r))
+        send(near, s, src, slot(r))
+        total[v] = len(eng)
+        wait("g", (v, total[v]))
+        theirs = slot(T.rank_of(partner))
+        send(near, s, theirs, theirs)
+        total[s] = 2 * len(eng) * len(near)
         wrote[key] = (s, total[s])
+        wrote[key + "v"] = (v, total[v])
 
     V, S, P = g.vector, g.scalar, g.tensor
 
@@ -131,9 +142,12 @@ def rank_program(g, core, T, topo):
     def make_cc(t):
         act([T.p6, T.p7][t % 2][:, L:2 * L], T.m2[:], F.Relu, K - M * (t + 1) - BIG, 1.0, ["m2"], ["cc%d" % (t % 2)], [6 + t % 2])
 
-    def lanes_down(out, lhs, rhs, rd, wr, b):
-        for p in range(16):
+    def lanes_down(out, lhs, rhs, rd, wr, b, ps):
+        for p in ps:
             mm(out, lhs[:, 15 - p:143 - p], rhs[:, p:L:16], p == 0, p == 15, rd, wr, [b], p == 15)
+
+    def tab_slot(s):
+        return lambda q: T.tab[:, sec(s) + L * q:sec(s) + L * (q + 1)]
 
     dma("s", T.coli[:], T.col[:], [], ["col"])
     dma("a", T.omi[:], T.om[:], [], ["om"])
@@ -146,12 +160,12 @@ def rank_program(g, core, T, topo):
     op("g", lambda: g.affine_select(T.e1[:], T.ones[0:8, 0:128], [[1, 128]], A.is_ge, 0.0, 0, -16), ["ones"], ["e1"])
     op("g", lambda: g.affine_select(T.ey[:, 128:272], T.ones[0:8, :], [[1, 144]], A.is_equal, 0.0, -15, -16), ["ones"], ["ey1"])
     op("g", lambda: g.affine_select(T.ey[:, 0:128], T.e1[:], [[-1, 128]], A.is_ge, 0.0, 15, 16), ["e1"], ["ey0"])
-    mine = T.tab[:, sec(0) + L * r:sec(0) + L * (r + 1)]
+    op("g", lambda: g.iota(T.m1[:], [[1, L]], int(BIG) + L * r, 0, allow_small_or_imprecise_dtypes=True), [], ["m1"])
+    mine = tab_slot(0)(r)
     ts(mp, T.omi[:], 1.0 / 8192, None, A.mult, None, ["om"], both("mp"), [0])
     tt(mine, T.coli[:], mp, A.add, ["col"] + both("mp"), ["own0"], [0])
-    spread(mine, mine, ["own0"], "far0")
+    spread(mine, tab_slot(0), ["own0"], "far0")
 
-    op("g", lambda: g.iota(T.m1[:], [[1, L]], int(BIG) + L * r, 0, allow_small_or_imprecise_dtypes=True), [], ["m1"])
     op("g", lambda: g.affine_select(T.ident[:], T.ones[:, 0:128], [[-1, 128]], A.is_equal, 0.0, 0, 1), ["ones"], ["ident"])
     ts(T.pi[:, 4:5], T.pi[:, 0:1], 15, None, A.bitwise_and, None, ["pi"], ["pj"])
     cp(jc, T.pi[:, 4:5], ["pj"], ["jc"])
@@ -183,7 +197,8 @@ def rank_program(g, core, T, topo):
     ts(bc, thc, -1.0 / 16, 1.0 / 32, A.mult, A.add, ["thc"], ["bc"])
     ts(T.cols[:, 4:5], thc, 61.0, -46.5, A.mult, A.add, ["thc"], ["c4"])
     ts(T.base[:], T.base[:], T.cols[:, 3:4], T.cols[:, 4:5], A.add, A.add, ["base", "j5", "c4"], ["base"])
-    lanes_down(T.p5[:, 0:16], T.zt, T.u1, ["zt"] + both("u1"), ["tl"], 5)
+    lanes_down(T.p5[:, 0:16], T.zt, T.u1, ["zt"] + both("u1"), ["tl"], 5, range(16))
+    tt(T.kn[:], T.u1[:], T.p6[:, L:2 * L], A.add, both("u1") + ["cc0"], both("kn"), [6])
 
     for t in range(RO):
         last = t == RO - 1
@@ -193,7 +208,7 @@ def rank_program(g, core, T, topo):
         tabs = ["own%d" % s for s in range(t + 1)] + ["far%d" % s for s in range(t + 1)]
         fs = both("f%d_" % t)
         for h in (1, 0):
-            i0, i1 = H * h, H * h + H
+            i0, i1 = CUT[h], CUT[h + 1]
             tt(T.tab[:, f0 + i0:f0 + i1], par.indirect(T.ol[:, i0 // 16:i1 // 16]), T.xs[:, i0:i1], A.max,
                ["own%d" % t, "far%d" % t, "ol", "xs"], [fs[h]])
             tt(T.zi[:, i0:i1], T.tab[:, f0 + i0:f0 + i1], T.p6[:, i0:i1], A.add, [fs[h], "dd"], ["zi%d" % h], [6])
@@ -203,34 +218,29 @@ def rank_program(g, core, T, topo):
                 tabs + fs[h:] + ["off%d" % h], ["ga%d" % h])
         xnew = T.tab[:, f0:f0 + L]
         if not last:
-            slot = T.tab[:, sec(t + 1) + L * r:sec(t + 1) + L * (r + 1)]
-            spread(xnew, slot, fs, "far%d" % (t + 1))
-            dma("s", slot, xnew, fs, ["own%d" % (t + 1)])
+            spread(xnew, tab_slot(t + 1), fs, "far%d" % (t + 1))
         if t == 0:
             ts(T.key[:], par.indirect(T.ol[:]), -8192.0, None, A.mult, None, ["own0", "far0", "ol"], ["key"])
             ts(T.qi[:], T.key[:], 4095, None, A.bitwise_and, None, ["key"], ["qi"])
             tt(T.tmp[:], T.qi[:], mp, A.max, ["qi"] + both("mp"), ["tmp"], [0])
             ts(lo, T.tmp[:], -1.0, 4096.0, A.mult, A.add, ["tmp"], ["lo"], [0])
-            ts(mp, T.tmp[:], 0.0, 12288.0, A.is_gt, A.mult, ["tmp"], both("mp"), [0])
-            tt(T.key[:], mp, T.tmp[:], A.add, both("mp") + ["tmp"], ["key"], [0])
-            tt(T.kn[:], T.u1[:], T.p6[:, L:2 * L], A.add, both("u1") + ["cc0"], both("kn"), [6])
         cp(T.gat[:, 0:16 * a], T.tab[:, f0:sec(t + 1)].indirect(T.off[:, 0:a]), tabs + fs + ["off0"], ["gv"])
         if t > 0:
-            w0 = M * (t - 1)
-            cp(T.ks[:], T.wt[:, w0 + L * r:w0 + L * (r + 1)], both("wown%d_" % t), ["ks"])
+            act(T.orr[:, L * t - L:L * t], T.p5[0:8, L:2 * L], F.Identity, -0.5, 1.0, ["rr"], ["orr"], [5])
         if not last:
-            tt(T.xs[:], xnew, ee, A.max, fs + ["ee"], ["xs"], [7])
+            act(tab_slot(t + 1)(r), xnew, F.Copy, 0.0, 1.0, fs, ["own%d" % (t + 1)])
             make_dd(t + 1)
             if t + 2 < RO:
                 make_cc(t + 1)
-                make_ee(t + 2)
+            if t > 0:
+                make_ee(t + 1)
         else:
-            ts(T.zi[:], xnew, -0.25, None, A.add, None, fs, both("zi"))
-            cp(T.ox[:], T.zi[:], both("zi"), ["ox"])
+            act(T.xs[:], xnew, F.Identity, WHOLE, 1.0, fs, ["xs"])
+            act(T.ox[:], T.xs[:], F.Identity, -WHOLE, 1.0, ["xs"], ["ox"])
             dma("s", T.yx[:], T.ox[:], ["ox"], [])
         if t > 0:
-            tt(T.key[:], T.wt[:, w0:w0 + M].indirect(T.ol[:]), T.ks[:], A.max,
-               both("wown%d_" % t) + both("wfar%d_" % t) + ["ol", "ks"], ["key"])
+            tt(T.key[:], T.wt[:, M * (t - 1):M * t].indirect(T.ol[:]), T.ks[:], A.max,
+               both("wown%d_" % t) + ["wfar%d" % t, "ol", "ks"], ["key"])
             ts(T.qi[:], T.key[:], int(K) - 1, None, A.bitwise_and, None, ["key"], ["qi"])
             ts(lo, T.qi[:], -1.0, K, A.mult, A.add, ["qi"], ["lo"], [0])
 
@@ -238,7 +248,7 @@ def rank_program(g, core, T, topo):
             return ["%s%d" % (k, h) for h in hs]
 
         def compare(hs, k):
-            i0, i1, b = H * hs[0], H * hs[-1] + H, 1 + hs[0]
+            i0, i1, b = CUT[hs[0]], CUT[hs[-1] + 1], 1 + hs[0]
             ck = hk("cmp%d_" % k, hs)
             tt(T.cmp[:, L * k + i0:L * k + i1], T.gat[:, 16 * i0 + k:16 * i1:16], T.p0[:, i0:i1], A.is_ge,
                hk("ga", hs) + (["gv"] if hs[0] == 0 else []) + ["lo"], ck, [0])
@@ -246,67 +256,64 @@ def rank_program(g, core, T, topo):
                ck + ["ident"], ["c%d" % b], [b], k == 15)
 
         def counted(hs, final):
-            i0, i1, b = H * hs[0], H * hs[-1] + H, 1 + hs[0]
-            if t > 0:
+            i0, i1, b = CUT[hs[0]], CUT[hs[-1] + 1], 1 + hs[0]
+            if last:
                 tt(T.u1[:, i0:i1], T.key[:, i0:i1], T.p0[:, i0:i1], A.add, ["key", "lo"], hk("u1", hs), [0])
-                if final and not last:
-                    lanes_down(T.p5[:, 0:16], T.zt, T.u1, ["zt"] + both("u1"), ["tl"], 5)
-            if last:
                 ts(T.tmp[:, i0:i1], T.p0[:, i0:i1], K, None, A.is_lt, None, ["lo"], hk("tmp", hs) + ["tmp"], [0])
-            ts(T.bb[:, i0:i1], [T.p1, T.p2][hs[0]][:, i0:i1], thc, bc, A.is_ge, A.add, ["c%d" % b, "thc", "bc"], hk("bb", hs), [b])
-            mm(T.p3[:, i0:i1], T.bo[:], T.bb[:, i0:i1], True, True, hk("bb", hs) + ["bo"], hk("sj", hs), [3])
-            if final and not last:
-                lanes_down(T.p4[:, 0:16], T.zs, T.bb, both("bb") + ["zs"], ["sl"], 4)
-            if last:
-                tt(T.kn[:, i0:i1], T.tmp[:, i0:i1], T.p0[:, i0:i1], A.mult, hk("tmp", hs) + ["lo"], hk("kn", hs), [0])
-                tt(T.p0[:, L + i0:L + i1], T.p7[:, i0:i1], T.kn[:, i0:i1], A.subtract, ["ee"] + hk("kn", hs), hk("mp", hs), [0, 7])
             elif t > 0:
                 tt(T.kn[:, i0:i1], T.u1[:, i0:i1], [T.p6, T.p7][t % 2][:, L + i0:L + i1], A.add,
                    hk("u1", hs) + ["cc%d" % (t % 2)], hk("kn", hs), [6 + t % 2])
+            ts(T.bb[:, i0:i1], [T.p1, T.p2][hs[0]][:, i0:i1], thc, bc, A.is_ge, A.add, ["c%d" % b, "thc", "bc"], hk("bb", hs), [b])
+            mm(T.p3[:, i0:i1], T.bo[:], T.bb[:, i0:i1], True, True, hk("bb", hs) + ["bo"], hk("sj", hs), [3])
+            if last:
+                tt(T.kn[:, i0:i1], T.tmp[:, i0:i1], T.p0[:, i0:i1], A.mult, hk("tmp", hs) + ["lo"], hk("kn", hs), [0])
+                tt(T.p0[:, L + i0:L + i1], T.p7[:, i0:i1], T.kn[:, i0:i1], A.subtract, ["ee"] + hk("kn", hs), hk("mp", hs), [0, 7])
+            elif final:
+                lanes_down(T.p4[:, 0:16], T.zs, T.bb, both("bb") + ["zs"], ["sl"], 4, range(16))
+                tt(T.xs[:], xnew, ee, A.max, fs + ["ee"], ["xs"], [7])
+                tt(T.ua[:, 0:16], T.p5[:, 0:16], T.base[:, 16 * t + 16:16 * t + 32], A.add, ["tl", "base"], ["u0"], [5])
 
-        def risen(hs):
-            i0, i1 = H * hs[0], H * hs[-1] + H
-            m = T.p0[:, L + i0:L + i1]
-            if not last:
-                wn = T.wt[:, M * t + L * r + i0:M * t + L * r + i1]
-                tt(m, T.p3[:, i0:i1], T.kn[:, i0:i1], A.min, hk("sj", hs) + hk("kn", hs), hk("mp", hs), [0, 3])
-                tt(wn, m, T.key[:, i0:i1], A.max, hk("mp", hs) + ["key"], hk("wown%d_" % (t + 1), hs), [0])
-                spread(wn, wn, hk("wown%d_" % (t + 1), hs), "wfar%d_%d" % (t + 1, hs[0]))
-            else:
-                ts(T.sb[:, i0:i1], T.p3[:, i0:i1], 0.0, None, A.is_gt, None, hk("sj", hs), hk("sb", hs), [3])
-                tt(m, T.sb[:, i0:i1], m, A.mult, hk("sb", hs) + hk("mp", hs), hk("mp", hs), [0])
-                tt(T.oo[:, i0:i1], m, T.kn[:, i0:i1], A.add, hk("mp", hs) + hk("kn", hs), hk("oo", hs), [0])
-                dma("s", T.yo[:, i0:i1], T.oo[:, i0:i1], hk("oo", hs), [])
-
-        if HALVES[t]:
+        if t == 0:
             for k in range(16):
                 compare([1], k)
             for k in range(16):
                 compare([0], k)
                 if k == 1:
                     counted([1], False)
-                if k == 3:
-                    risen([1])
+            ts(mp, T.tmp[:], 0.0, 12288.0, A.is_gt, A.mult, ["tmp"], both("mp"), [0])
+            tt(T.key[:], mp, T.tmp[:], A.add, both("mp") + ["tmp"], ["key"], [0])
             counted([0], True)
-            risen([0])
         else:
             for k in range(16):
                 compare([0, 1], k)
+                if not last and k == 0:
+                    tt(T.u1[:], T.key[:], lo, A.add, ["key", "lo"], both("u1"), [0])
+                if not last and k > 0:
+                    lanes_down(T.p5[:, 0:16], T.zt, T.u1, ["zt"] + both("u1"), ["tl"], 5, [0, 1] if k == 1 else [k])
             counted([0, 1], True)
-            risen([0, 1])
         if not last:
+            wown = T.wt[:, M * t + L * r:M * t + L * (r + 1)]
+            tt(mp, T.p3[:, 0:L], T.kn[:], A.min, both("sj") + both("kn"), both("mp"), [0, 3])
+            tt(wown, mp, T.key[:], A.max, both("mp") + ["key"], both("wown%d_" % (t + 1)), [0])
+            spread(wown, lambda q: T.wt[:, M * t + L * q:M * t + L * (q + 1)], both("wown%d_" % (t + 1)), "wfar%d" % (t + 1))
+            act(T.ks[:], wown, F.Copy, 0.0, 1.0, both("wown%d_" % (t + 1)), ["ks"])
             act(T.sb[:], T.p3[:, 0:L], F.Sign, 0.0, 1.0, both("sj"), both("sb"), [3])
-            tt(T.ua[:, 0:16], T.p5[:, 0:16], T.base[:, 16 * t + 16:16 * t + 32], A.add, ["tl", "base"], ["u0"], [5])
             ts(T.ua[:, 16:32], T.p4[:, 0:16], 0.0, 16.0, A.is_gt, A.mult, ["sl"], ["u1a"], [4])
             tt(T.ua[:, 32:48], T.p4[:, 0:16], T.ua[:, 0:16], A.add, ["sl", "u0"], ["u2"], [4])
             tt(T.ui[:, 0:16], T.ua[:, 16:32], T.ua[:, 32:48], A.add, ["u1a", "u2"], ["u4"])
             ts(T.ui[:, 16:32], T.ui[:, 0:16], M - 1, None, A.bitwise_and, None, ["u4"], ["u5"])
             cp(T.ol[:], T.ui[:, 16:32], ["u5"], ["ol"])
+        else:
+            ts(T.sb[:], T.p3[:, 0:L], 0.0, None, A.is_gt, None, both("sj"), both("sb"), [3])
+            tt(mp, T.sb[:], mp, A.mult, both("sb") + both("mp"), both("mp"), [0])
+            tt(T.oo[:], mp, T.kn[:], A.add, both("mp") + both("kn"), ["oo"], [0])
+            dma("s", T.yo[:], T.oo[:], ["oo"], [])
         rr = T.p5[0:8, L:2 * L]
         n = 2 if last else 1
         mm(rr, T.et[:, 0:8], T.u1[:], True, False, ["et0"] + both("u1"), ["rr"], [5], False)
         mm(rr, T.et[:, 8 * n:8 * n + 8], T.sb[:], False, True, ["et%d" % n] + both("sb"), ["rr"], [5])
-        act(T.orr[:, L * t:L * t + L], rr, F.Identity, -1.0 if last else -0.5, 1.0, ["rr"], ["orr"], [5])
+        if last:
+            act(T.orr[:, L * t:L * t + L], rr, F.Identity, -1.0, 1.0, ["rr"], ["orr"], [5])
     dma("a", T.yr[:], T.orr[:], ["orr"], [])
     for s in total:
         wait("g", (s, total[s]))

@@ -2,26 +2,28 @@ from concourse.bass import DstId, RemoteDMATransfer
 from concourse.mybir import AluOpType, ActivationFunctionType
 
 L, M, RO = 256, 2048, 4
-CUT = [0, 128, L]
 K = 16384.0
 BIG = 65536.0
 WHOLE = 12582912.0
-FR = 1024
-SPLIT = [32, 100, 100, 100]
+HEAD = 64
+GATHER = [[0, 64, 128, 192, 232]] + 3 * [[0, 64, 128, 176]]
+SHARE = [[232, 256]] + 3 * [[176, 256]]
+COMPARE = [[0, 64, 128, 192, 256]] + 2 * [[0, 96, 224]] + [[0, 96, 160, 224]]
+HALF = 128
 
 SCRATCH = {"p%d" % b: ("psum", [128, 512], "float32") for b in range(8)}
 for dtype, tiles in (
-        ("float32", dict(tab=FR + 4 * M, wt=3 * M, gat=16 * L, cols=8, base=64, one=L, m1=L, m2=L, xs=L, ks=L, ua=48,
-                         tmp=L, kn=L, ox=L, oo=L)),
-        ("bfloat16", dict(cmp=16 * L, ones=144, ident=128, bo=128, zs=144, zt=144, et=24, u1=L, bb=L, sb=L)),
+        ("float32", dict(tab=4 * M + L, ft=3 * M, gat=16 * L, zero=3 * L, cols=8, base=96, ys=L, ks=L, ua=48, tmp=L, kn=L,
+                         ox=L, oo=L, eyef=128, m1=L, m2=L, lev=L, nl=L, cs=L)),
+        ("bfloat16", dict(cmp=16 * L, signs=16 * 64, ones=L, eye=128, bo=128, zs=144, et=16, bu=2 * L, lim=L, sb=L)),
         ("int32", dict(coli=L, omi=L, pi=8, zi=L, ui=32, key=L, qi=L)),
         ("uint16", dict(off=L, ol=16))):
     SCRATCH.update({name: ("sbuf", [128, n], dtype) for name, n in tiles.items()})
 SCRATCH.update({"mti": ("sbuf", [8, 264], "int32"), "mtb": ("sbuf", [8, 264], "bfloat16"),
                 "e1": ("sbuf", [8, 128], "bfloat16"), "ey": ("sbuf", [8, 272], "bfloat16"),
-                "orr": ("sbuf", [8, RO * L], "float32")})
+                "orr": ("sbuf", [8, 3 * L], "float32")})
 SEMAPHORES = (["qv", "qa", "qt", "qg", "sent"] + ["arr%d" % k for k in range(7)] + ["via%d" % k for k in range(7)]
-              + ["dma%d" % k for k in range(7)])
+              + ["dma%d" % k for k in range(9)])
 
 A = AluOpType
 F = ActivationFunctionType
@@ -117,203 +119,256 @@ def rank_program(g, core, T, topo):
     def cp(out, in_, rd, wr, banks=()):
         op("v", lambda: V.tensor_copy(out, in_), rd, wr, banks)
 
+    def fill(out, value, wr):
+        op("v", lambda: V.memset(out, value), [], wr)
+
     def act(out, in_, f, bias, scale, rd, wr, banks=()):
         op("a", lambda: S.activation(out, in_, f, bias=bias, scale=scale), rd, wr, banks)
 
     def mm(out, lhsT, rhs, start, stop, rd, wr, banks, inc=True):
         op("t", lambda: P.matmul(out, lhsT, rhs, start, stop), rd, wr, banks, inc)
 
-    def sec(s):
-        return FR + M * s
+    def names(k, i0, i1):
+        return ["%s@%d" % (k, b) for b in range(i0 // 8, (i1 + 7) // 8)]
 
-    def both(k):
-        return [k + "0", k + "1"]
+    def full(k):
+        return names(k, 0, L)
 
-    lo, mp = T.p0[:, 0:L], T.p0[:, L:2 * L]
-    dd, ee = T.p6[:, 0:L], T.p7[:, 0:L]
-    thc, bc, jc = T.cols[:, 0:1], T.cols[:, 1:2], T.cols[:, 2:3]
+    def pairs(cuts):
+        return list(zip(cuts, cuts[1:]))
 
-    def make_dd(t):
-        act(dd, T.one[:], F.Identity, L * (t + 1) - 0.25, -float(M * (t + 1) + L * r + L * (t + 1)), ["one"], ["dd"], [6])
+    def slots(buf, c0):
+        return lambda q: buf[:, c0 + L * q:c0 + L * (q + 1)]
 
-    def make_ee(t):
-        act(ee, T.m1[:], F.Relu, M * (t + 1) - BIG, 1.0, ["m1"], ["ee"], [7])
+    lo, mp, sj, sl, rr = T.p0[:, 0:L], T.p0[:, L:2 * L], T.p3[:, 0:L], T.p4[:, 0:32], T.p5[0:8, 0:L]
+    step, shift, cc, bb, u1 = T.p6[:, 0:L], T.p6[:, L:2 * L], T.p7[:, 0:L], T.bu[:, 0:L], T.bu[:, L:2 * L]
+    thc, bc, jc, j5 = T.cols[:, 0:1], T.cols[:, 1:2], T.cols[:, 2:3], T.cols[:, 3:4]
 
     def make_cc(t):
-        act([T.p6, T.p7][t % 2][:, L:2 * L], T.m2[:], F.Relu, K - M * (t + 1) - BIG, 1.0, ["m2"], ["cc%d" % (t % 2)], [6 + t % 2])
+        act(cc, T.m2[:], F.Relu, K - M * (t + 1) - BIG, 1.0, ["m2"], ["cc"], [7])
 
-    def lanes_down(out, lhs, rhs, rd, wr, b, ps):
-        for p in ps:
-            mm(out, lhs[:, 15 - p:143 - p], rhs[:, p:L:16], p == 0, p == 15, rd, wr, [b], p == 15)
-
-    def tab_slot(s):
-        return lambda q: T.tab[:, sec(s) + L * q:sec(s) + L * (q + 1)]
-
-    dma("s", T.coli[:], T.col[:], [], ["col"])
     dma("a", T.omi[:], T.om[:], [], ["om"])
+    dma("s", T.coli[:], T.col[:], [], ["col"])
     dma("s", T.mti[:, 0:L], T.mem[:], [], ["mem"])
     dma("a", T.mti[:, L:L + 1], T.th[:], [], ["th"])
-    op("v", lambda: V.memset(T.ones[:], 1.0), [], ["ones"])
-    op("v", lambda: V.memset(T.u1[:], K), [], both("u1"))
+    fill(T.ones[:], 1.0, ["ones"])
     op("g", lambda: g.iota(T.pi[:, 0:1], [[0, 1]], 0, 1), [], ["pi"])
-    op("g", lambda: g.iota(T.base[:], [[77, 4], [80, 16]], L * r, 0, allow_small_or_imprecise_dtypes=True), [], ["base"])
+    op("g", lambda: g.iota(T.ua[:], [[77, 3], [80, 16]], L * r + 77, 0, allow_small_or_imprecise_dtypes=True), [], ["base"])
     op("g", lambda: g.affine_select(T.e1[:], T.ones[0:8, 0:128], [[1, 128]], A.is_ge, 0.0, 0, -16), ["ones"], ["e1"])
-    op("g", lambda: g.affine_select(T.ey[:, 128:272], T.ones[0:8, :], [[1, 144]], A.is_equal, 0.0, -15, -16), ["ones"], ["ey1"])
+    op("g", lambda: g.affine_select(T.ey[:, 128:272], T.ones[0:8, 0:144], [[1, 144]], A.is_equal, 0.0, -15, -16), ["ones"], ["ey1"])
     op("g", lambda: g.affine_select(T.ey[:, 0:128], T.e1[:], [[-1, 128]], A.is_ge, 0.0, 15, 16), ["e1"], ["ey0"])
-    op("g", lambda: g.iota(T.m1[:], [[1, L]], int(BIG) + L * r, 0, allow_small_or_imprecise_dtypes=True), [], ["m1"])
-    mine = tab_slot(0)(r)
-    ts(mp, T.omi[:], 1.0 / 8192, None, A.mult, None, ["om"], both("mp"), [0])
-    tt(mine, T.coli[:], mp, A.add, ["col"] + both("mp"), ["own0"], [0])
-    spread(mine, tab_slot(0), ["own0"], "far0")
-
-    op("g", lambda: g.affine_select(T.ident[:], T.ones[:, 0:128], [[-1, 128]], A.is_equal, 0.0, 0, 1), ["ones"], ["ident"])
+    fill(u1, K, ["u1"])
     ts(T.pi[:, 4:5], T.pi[:, 0:1], 15, None, A.bitwise_and, None, ["pi"], ["pj"])
+    fill(T.base[:], 0.0, ["bs"])
+    ts(j5, T.pi[:, 4:5], 5.0, None, A.mult, None, ["pj"], ["j5"])
     cp(jc, T.pi[:, 4:5], ["pj"], ["jc"])
-    ts(T.cols[:, 3:4], T.pi[:, 4:5], 5.0, None, A.mult, None, ["pj"], ["j5"])
-    cp(T.mtb[:, 0:L + 1], T.mti[:, 0:L + 1], ["mem", "th"], ["mtb"])
-    mm(T.p1[:, 0:272], T.ey[:, 0:128], T.ey[:], True, True, ["ey0", "ey1"], ["c1"], [1])
-    mm(T.p2[:, 0:L + 1], T.ey[:, 0:128], T.mtb[:, 0:L + 1], True, True, ["ey0", "mtb"], ["c2"], [2])
-    ts(T.ui[:, 0:16], T.base[:, 0:16], T.cols[:, 3:4], None, A.add, None, ["base", "j5"], ["u4"])
+    ts(T.cols[:, 4:5], T.pi[:, 4:5], 5.0, -16.0, A.mult, A.add, ["pj"], ["c4"])
+    ts(T.ui[:, 0:16], T.ua[:, 0:16], j5, -77.0, A.add, A.add, ["base", "j5"], ["u4"])
+    for t in range(RO - 1):
+        ts(T.base[:, 32 * t + 16:32 * t + 32], T.ua[:, 16 * t:16 * t + 16], T.cols[:, 4:5], K, A.add, A.mult,
+           ["base", "c4", "bs"], ["bs%d" % t])
     ts(T.ui[:, 16:32], T.ui[:, 0:16], M - 1, None, A.bitwise_and, None, ["u4"], ["u5"])
+    mine = slots(T.tab, 0)(r)
+    ts(mp, T.omi[:], 1.0 / 8192, None, A.mult, None, ["om"], full("mp"), [0])
     cp(T.ol[:], T.ui[:, 16:32], ["u5"], ["ol"])
-    ts(T.one[:], T.p2[:, 0:L], jc, None, A.is_equal, None, ["c2", "jc"], ["one"], [2])
-    cp(thc, T.p2[:, L:L + 1], ["c2"], ["thc"], [2])
-    ts(T.m2[:], T.m1[:], -1.0, 2 * BIG, A.mult, A.add, ["m1"], ["m2"])
-    tt(T.m1[:], T.m1[:], T.one[:], A.mult, ["m1", "one"], ["m1"])
-    make_dd(0)
-    make_ee(0)
-    tt(T.m2[:], T.m2[:], T.one[:], A.mult, ["m2", "one"], ["m2"])
-    tt(T.xs[:], mine, ee, A.max, ["own0", "ee"], ["xs"], [7])
+    tt(mine, T.coli[:], mp, A.add, ["col"] + full("mp"), ["own0"], [0])
+    op("g", lambda: g.iota(T.lev[:], [[1, L]], int(BIG) + L * r, 0, allow_small_or_imprecise_dtypes=True), [], ["lev"])
+    spread(mine, slots(T.tab, 0), ["own0"], "far0")
+
+    op("g", lambda: g.affine_select(T.eye[:], T.ones[:, 0:128], [[-1, 128]], A.is_equal, 0.0, 0, 1), ["ones"], ["eye"])
+    cp(T.mtb[:, 0:L + 1], T.mti[:, 0:L + 1], ["mem", "th"], ["mtb"])
+    mm(T.p1[:, 0:272], T.ey[:, 0:128], T.ey[:], True, True, ["ey0", "ey1"], ["blk"], [1])
+    mm(T.p3[:, 0:L + 1], T.ey[:, 0:128], T.mtb[:, 0:L + 1], True, True, ["ey0", "mtb"], ["mt"], [3])
+    act(T.m1[:], T.lev[:], F.Identity, 0.0, 1.0 / M, ["lev"], ["m1"])
+    act(T.m2[:], T.lev[:], F.Identity, 2 * BIG / M, -1.0 / M, ["lev"], ["m2"])
+    act(T.bo[:], T.p1[:, 0:128], F.Copy, 0.0, 16.0, ["blk"], ["bo"], [1])
+    act(T.zs[:], T.p1[:, 128:272], F.Copy, 0.0, 1.0, ["blk"], ["zs"], [1])
+    for n, wgt in enumerate([1.0 / (16 * K), 1.0 / 32]):
+        act(T.et[:, 8 * n:8 * n + 8], T.p1[:, 0:128:16], F.Copy, 0.0, wgt, ["blk"], ["et%d" % n], [1])
+    ts(T.zi[:], T.omi[:], -1.0, None, A.mult, None, ["om"], ["zi"])
+    ts(step, T.p3[:, 0:L], jc, float(M), A.is_equal, A.mult, ["mt", "jc"], ["step"], [3, 6])
+    ts(T.qi[:], T.zi[:], 4095, None, A.bitwise_and, None, ["zi"], full("qi"))
+    tt(T.m1[:], T.m1[:], step, A.mult, ["m1", "step"], ["m1"], [6])
+    cp(thc, T.p3[:, L:L + 1], ["mt"], ["thc"], [3])
+    act(cc, T.m1[:], F.Relu, M - L * r - BIG, 1.0, ["m1"], ["cc"], [7])
+    cp(mp, T.qi[:], full("qi"), full("mp"), [0])
+    tt(T.m2[:], T.m2[:], step, A.mult, ["m2", "step"], ["m2"], [6])
+    ts(shift, T.p3[:, 0:L], jc, float(L * r), A.is_equal, A.mult, ["mt", "jc"], ["shift"], [3, 6])
+    ts(T.cols[:, 5:6], thc, -0.5, -16 * 61 * K, A.add, A.mult, ["thc"], ["c5"])
+    ts(bc, thc, 61 * K, None, A.mult, None, ["thc"], ["bc"])
+    ts(T.cols[:, 6:7], thc, 2.0, -16.0, A.mult, A.add, ["thc"], ["c6"])
+    tt(T.ys[:], mine, cc, A.max, ["own0", "cc"], ["ys"], [7])
+    act(T.lim[:], T.ones[:], F.Identity, 0.0, T.cols[:, 5:6], ["ones", "c5"], ["lim"])
+    act(T.eyef[:], T.eye[:], F.Copy, 0.0, 1.0, ["eye"], ["eyef"])
     make_cc(0)
-    make_ee(1)
-    ts(T.zi[:], T.omi[:], -1.0, None, A.mult, None, ["om"], both("zi"))
-    ts(T.qi[:], T.zi[:], 4095, None, A.bitwise_and, None, both("zi"), ["qi"])
-    cp(mp, T.qi[:], ["qi"], both("mp"), [0])
-    ts(T.bo[:], T.p1[:, 0:128], 131072.0, None, A.mult, None, ["c1"], ["bo"], [1])
-    ts(T.zs[:], T.p1[:, 128:272], 61.0, None, A.mult, None, ["c1"], ["zs"], [1])
-    ts(T.zt[:], T.p1[:, 128:272], 1.0 / K, None, A.mult, None, ["c1"], ["zt"], [1])
-    for n, wgt in enumerate([1.0 / (16 * K), 1.0 / 32, 1.0 / 16]):
-        ts(T.et[:, 8 * n:8 * n + 8], T.p1[:, 0:128:16], wgt, None, A.mult, None, ["c1"], ["et%d" % n], [1])
-    ts(bc, thc, -1.0 / 16, 1.0 / 32, A.mult, A.add, ["thc"], ["bc"])
-    ts(T.cols[:, 4:5], thc, 61.0, -46.5, A.mult, A.add, ["thc"], ["c4"])
-    ts(T.base[:], T.base[:], T.cols[:, 3:4], T.cols[:, 4:5], A.add, A.add, ["base", "j5", "c4"], ["base"])
-    lanes_down(T.p5[:, 0:16], T.zt, T.u1, ["zt"] + both("u1"), ["tl"], 5, range(16))
-    tt(T.kn[:], T.u1[:], T.p6[:, L:2 * L], A.add, both("u1") + ["cc0"], both("kn"), [6])
 
     for t in range(RO):
         last = t == RO - 1
-        f0 = FR - L * (t + 1)
-        a = SPLIT[t]
-        par = T.tab[:, sec(t):sec(t + 1)]
-        tabs = ["own%d" % s for s in range(t + 1)] + ["far%d" % s for s in range(t + 1)]
-        fs = both("f%d_" % t)
-        for h in (1, 0):
-            i0, i1 = CUT[h], CUT[h + 1]
-            tt(T.tab[:, f0 + i0:f0 + i1], par.indirect(T.ol[:, i0 // 16:i1 // 16]), T.xs[:, i0:i1], A.max,
-               ["own%d" % t, "far%d" % t, "ol", "xs"], [fs[h]])
-            tt(T.zi[:, i0:i1], T.tab[:, f0 + i0:f0 + i1], T.p6[:, i0:i1], A.add, [fs[h], "dd"], ["zi%d" % h], [6])
-            ts(T.off[:, i0:i1], T.zi[:, i0:i1], -float(i0), None, A.add, None, ["zi%d" % h], ["off%d" % h])
-            c0 = max(i0, a)
-            act(T.gat[:, 16 * c0:16 * i1], T.tab[:, f0 + i0:sec(t + 1)].indirect(T.off[:, c0:i1]), F.Copy, 0.0, 1.0,
-                tabs + fs[h:] + ["off%d" % h], ["ga%d" % h])
-        xnew = T.tab[:, f0:f0 + L]
-        if not last:
-            spread(xnew, tab_slot(t + 1), fs, "far%d" % (t + 1))
+        e0 = M * (t + 1)
+        par = T.tab[:, M * t:e0]
+        tabs = ["own%d" % s for s in range(t + 1)] + ["far%d" % s for s in range(t + 1)] + ["zero%d" % s for s in range(1, t + 1)]
+        y, fs = T.tab[:, e0:e0 + L], ["y%d_0" % t, "y%d_1" % t]
+        heads = ((0, 0, HEAD), (1, HEAD, L))
+        for h, i0, i1 in heads:
+            tt(T.tab[:, e0 + i0:e0 + i1], par.indirect(T.ol[:, i0 // 16:i1 // 16]), T.ys[:, i0:i1], A.max,
+               tabs[t::t + 1][:2] + tabs[-1:] + ["ol", "ys"], [fs[h]])
+        for h, i0, i1 in heads:
+            cp(T.off[:, i0:i1], T.tab[:, e0 + i0:e0 + i1], [fs[h]], ["off%d" % h])
+            for c0, c1 in pairs(GATHER[t]):
+                if i0 <= c0 < i1:
+                    act(T.gat[:, 16 * c0:16 * c1], T.tab[:, 0:e0 + i1].indirect(T.off[:, c0:c1]), F.Copy, 0.0, 1.0,
+                        tabs + fs[:h + 1] + ["off%d" % h], names("ga", c0, c1))
+            if t == 0 and h == 0:
+                ts(T.key[:], par.indirect(T.ol[:]), -8192.0, None, A.mult, None, ["own0", "far0", "ol"], full("key"))
         if t == 0:
-            ts(T.key[:], par.indirect(T.ol[:]), -8192.0, None, A.mult, None, ["own0", "far0", "ol"], ["key"])
-            ts(T.qi[:], T.key[:], 4095, None, A.bitwise_and, None, ["key"], ["qi"])
-            tt(T.tmp[:], T.qi[:], mp, A.max, ["qi"] + both("mp"), ["tmp"], [0])
-            ts(lo, T.tmp[:], -1.0, 4096.0, A.mult, A.add, ["tmp"], ["lo"], [0])
-        cp(T.gat[:, 0:16 * a], T.tab[:, f0:sec(t + 1)].indirect(T.off[:, 0:a]), tabs + fs + ["off0"], ["gv"])
-        if t > 0:
-            act(T.orr[:, L * t - L:L * t], T.p5[0:8, L:2 * L], F.Identity, -0.5, 1.0, ["rr"], ["orr"], [5])
-        if not last:
-            act(tab_slot(t + 1)(r), xnew, F.Copy, 0.0, 1.0, fs, ["own%d" % (t + 1)])
-            make_dd(t + 1)
-            if t + 2 < RO:
-                make_cc(t + 1)
-            if t > 0:
-                make_ee(t + 1)
-        else:
-            act(T.xs[:], xnew, F.Identity, WHOLE, 1.0, fs, ["xs"])
-            act(T.ox[:], T.xs[:], F.Identity, -WHOLE, 1.0, ["xs"], ["ox"])
-            dma("s", T.yx[:], T.ox[:], ["ox"], [])
-        if t > 0:
-            tt(T.key[:], T.wt[:, M * (t - 1):M * t].indirect(T.ol[:]), T.ks[:], A.max,
-               both("wown%d_" % t) + ["wfar%d" % t, "ol", "ks"], ["key"])
-            ts(T.qi[:], T.key[:], int(K) - 1, None, A.bitwise_and, None, ["key"], ["qi"])
-            ts(lo, T.qi[:], -1.0, K, A.mult, A.add, ["qi"], ["lo"], [0])
+            ts(T.qi[:], T.key[:], 4095, None, A.bitwise_and, None, full("key"), full("qi"))
 
-        def hk(k, hs):
-            return ["%s%d" % (k, h) for h in hs]
+        def slot(q):
+            return slots(T.zero, L * t)(0) if q == 0 else slots(T.tab, e0)(q)
 
-        def compare(hs, k):
-            i0, i1, b = CUT[hs[0]], CUT[hs[-1] + 1], 1 + hs[0]
-            ck = hk("cmp%d_" % k, hs)
-            tt(T.cmp[:, L * k + i0:L * k + i1], T.gat[:, 16 * i0 + k:16 * i1:16], T.p0[:, i0:i1], A.is_ge,
-               hk("ga", hs) + (["gv"] if hs[0] == 0 else []) + ["lo"], ck, [0])
-            mm([T.p1, T.p2][hs[0]][:, i0:i1], T.ident[:], T.cmp[:, L * k + i0:L * k + i1], k == 0, k == 15,
-               ck + ["ident"], ["c%d" % b], [b], k == 15)
+        def share(n):
+            if n < len(SHARE[t]) - 1:
+                c0, c1 = SHARE[t][n:n + 2]
+                cp(T.gat[:, 16 * c0:16 * c1], T.tab[:, 0:e0 + L].indirect(T.off[:, c0:c1]), tabs + fs + ["off1"], names("ga", c0, c1))
 
-        def counted(hs, final):
-            i0, i1, b = CUT[hs[0]], CUT[hs[-1] + 1], 1 + hs[0]
-            if last:
-                tt(T.u1[:, i0:i1], T.key[:, i0:i1], T.p0[:, i0:i1], A.add, ["key", "lo"], hk("u1", hs), [0])
-                ts(T.tmp[:, i0:i1], T.p0[:, i0:i1], K, None, A.is_lt, None, ["lo"], hk("tmp", hs) + ["tmp"], [0])
-            elif t > 0:
-                tt(T.kn[:, i0:i1], T.u1[:, i0:i1], [T.p6, T.p7][t % 2][:, L + i0:L + i1], A.add,
-                   hk("u1", hs) + ["cc%d" % (t % 2)], hk("kn", hs), [6 + t % 2])
-            ts(T.bb[:, i0:i1], [T.p1, T.p2][hs[0]][:, i0:i1], thc, bc, A.is_ge, A.add, ["c%d" % b, "thc", "bc"], hk("bb", hs), [b])
-            mm(T.p3[:, i0:i1], T.bo[:], T.bb[:, i0:i1], True, True, hk("bb", hs) + ["bo"], hk("sj", hs), [3])
-            if last:
-                tt(T.kn[:, i0:i1], T.tmp[:, i0:i1], T.p0[:, i0:i1], A.mult, hk("tmp", hs) + ["lo"], hk("kn", hs), [0])
-                tt(T.p0[:, L + i0:L + i1], T.p7[:, i0:i1], T.kn[:, i0:i1], A.subtract, ["ee"] + hk("kn", hs), hk("mp", hs), [0, 7])
-            elif final:
-                lanes_down(T.p4[:, 0:16], T.zs, T.bb, both("bb") + ["zs"], ["sl"], 4, range(16))
-                tt(T.xs[:], xnew, ee, A.max, fs + ["ee"], ["xs"], [7])
-                tt(T.ua[:, 0:16], T.p5[:, 0:16], T.base[:, 16 * t + 16:16 * t + 32], A.add, ["tl", "base"], ["u0"], [5])
+        def onward():
+            if not last:
+                tt(T.ys[:], y, step, A.add, fs + ["step"], ["ys"], [6])
 
-        if t == 0:
-            for k in range(16):
-                compare([1], k)
-            for k in range(16):
-                compare([0], k)
-                if k == 1:
-                    counted([1], False)
-            ts(mp, T.tmp[:], 0.0, 12288.0, A.is_gt, A.mult, ["tmp"], both("mp"), [0])
-            tt(T.key[:], mp, T.tmp[:], A.add, both("mp") + ["tmp"], ["key"], [0])
-            counted([0], True)
-        else:
-            for k in range(16):
-                compare([0, 1], k)
-                if not last and k == 0:
-                    tt(T.u1[:], T.key[:], lo, A.add, ["key", "lo"], both("u1"), [0])
-                if not last and k > 0:
-                    lanes_down(T.p5[:, 0:16], T.zt, T.u1, ["zt"] + both("u1"), ["tl"], 5, [0, 1] if k == 1 else [k])
-            counted([0, 1], True)
-        if not last:
-            wown = T.wt[:, M * t + L * r:M * t + L * (r + 1)]
-            tt(mp, T.p3[:, 0:L], T.kn[:], A.min, both("sj") + both("kn"), both("mp"), [0, 3])
-            tt(wown, mp, T.key[:], A.max, both("mp") + ["key"], both("wown%d_" % (t + 1)), [0])
-            spread(wown, lambda q: T.wt[:, M * t + L * q:M * t + L * (q + 1)], both("wown%d_" % (t + 1)), "wfar%d" % (t + 1))
-            act(T.ks[:], wown, F.Copy, 0.0, 1.0, both("wown%d_" % (t + 1)), ["ks"])
-            act(T.sb[:], T.p3[:, 0:L], F.Sign, 0.0, 1.0, both("sj"), both("sb"), [3])
-            ts(T.ua[:, 16:32], T.p4[:, 0:16], 0.0, 16.0, A.is_gt, A.mult, ["sl"], ["u1a"], [4])
-            tt(T.ua[:, 32:48], T.p4[:, 0:16], T.ua[:, 0:16], A.add, ["sl", "u0"], ["u2"], [4])
-            tt(T.ui[:, 0:16], T.ua[:, 16:32], T.ua[:, 32:48], A.add, ["u1a", "u2"], ["u4"])
-            ts(T.ui[:, 16:32], T.ui[:, 0:16], M - 1, None, A.bitwise_and, None, ["u4"], ["u5"])
-            cp(T.ol[:], T.ui[:, 16:32], ["u5"], ["ol"])
-        else:
-            ts(T.sb[:], T.p3[:, 0:L], 0.0, None, A.is_gt, None, both("sj"), both("sb"), [3])
-            tt(mp, T.sb[:], mp, A.mult, both("sb") + both("mp"), both("mp"), [0])
-            tt(T.oo[:], mp, T.kn[:], A.add, both("mp") + both("kn"), ["oo"], [0])
-            dma("s", T.yo[:], T.oo[:], ["oo"], [])
-        rr = T.p5[0:8, L:2 * L]
-        n = 2 if last else 1
-        mm(rr, T.et[:, 0:8], T.u1[:], True, False, ["et0"] + both("u1"), ["rr"], [5], False)
-        mm(rr, T.et[:, 8 * n:8 * n + 8], T.sb[:], False, True, ["et%d" % n] + both("sb"), ["rr"], [5])
         if last:
-            act(T.orr[:, L * t:L * t + L], rr, F.Identity, -1.0, 1.0, ["rr"], ["orr"], [5])
-    dma("a", T.yr[:], T.orr[:], ["orr"], [])
+            tt(T.ox[:], y, shift, A.add, fs + ["shift"], ["ox"], [6])
+        elif r == 0:
+            spread(y, slot, fs, "far%d" % (t + 1))
+        else:
+            tt(slot(r), y, shift, A.add, fs + ["shift"], ["own%d" % (t + 1)], [6])
+            spread(slot(r), slot, ["own%d" % (t + 1)], "far%d" % (t + 1))
+        top = COMPARE[t][-1]
+        cut = COMPARE[t][-2] if last else HALF
+        parts = [(0, cut, 3, T.p3), (cut, L, 3, T.p3) if last else (cut, L, 2, T.p2)]
+
+        def limit(i0, i1, b, pb):
+            mm(pb[:, i0:i1], T.eye[:], T.lim[:, i0:i1], True, False, ["eye", "lim"], names("sj", i0, i1), [b], False)
+
+        for part in parts[:1] if last else parts:
+            limit(*part)
+        if not last:
+            mm(sl, T.eyef[:], T.base[:, 32 * t:32 * t + 32], True, False, ["eyef", "bs%d" % t], ["sl"], [4], False)
+        if t == 0:
+            tt(T.tmp[:], T.qi[:], mp, A.max, full("qi") + full("mp"), ["tmp"], [0])
+            share(0)
+            ts(lo, T.tmp[:], -1.0, 4096.0, A.mult, A.add, ["tmp"], full("lo"), [0])
+            onward()
+        else:
+            onward()
+            share(0)
+            two = pairs([0, COMPARE[t][1], L])
+            for i0, i1 in two:
+                tt(T.key[:, i0:i1], T.ft[:, M * (t - 1):M * t].indirect(T.ol[:, i0 // 16:i1 // 16]), T.ks[:, i0:i1], A.max,
+                   ["fown%d_0" % (t - 1), "fown%d_1" % (t - 1), "ffar%d" % (t - 1), "ks", "ol"], names("key", i0, i1))
+            for i0, i1 in two:
+                ts(T.qi[:, i0:i1], T.key[:, i0:i1], int(K) - 1, None, A.bitwise_and, None, names("key", i0, i1), names("qi", i0, i1))
+            ts(T.p0[:, 0:two[0][1]], T.qi[:, 0:two[0][1]], -1.0, K, A.mult, A.add, names("qi", *two[0]), names("lo", *two[0]), [0])
+            if top < L:
+                ts(T.nl[:, top:L], T.qi[:, top:L], 0.5 - K, None, A.add, None, names("qi", top, L), ["nl"])
+            ts(T.p0[:, two[0][1]:L], T.qi[:, two[0][1]:L], -1.0, K, A.mult, A.add, names("qi", *two[1]), names("lo", *two[1]), [0])
+        for i in range(top, L):
+            op("a", lambda: S.activation(T.signs[:, 16 * (i - top):16 * (i - top + 1)], T.gat[:, 16 * i:16 * i + 16], F.Sign,
+                                         bias=T.nl[:, i:i + 1], scale=1.0, accum_out=T.cs[:, i:i + 1]),
+               names("ga", top, L) + ["nl"], ["cs"] if i == L - 1 else [], (), i == L - 1)
+        if last:
+            act(T.ys[:], T.ox[:], F.Identity, WHOLE, 1.0, ["ox"], ["ys"])
+            act(T.orr[:, L * t - L:L * t], rr, F.Identity, -0.5, 1.0, ["rr"], ["orr"], [5])
+            act(T.ox[:], T.ys[:], F.Identity, -WHOLE, 1.0, ["ys"], ["ox"])
+            dma("s", T.yr[:, 0:L * t], T.orr[:], ["orr"], [])
+            dma("s", T.yx[:], T.ox[:], ["ox"], [])
+        else:
+            if t > 0:
+                act(T.orr[:, L * t - L:L * t], rr, F.Identity, -0.5, 1.0, ["rr"], ["orr"], [5])
+            if r > 0:
+                act(y, slot(0), F.Copy, 0.0, 1.0, ["far%d" % (t + 1)], fs + ["zero%d" % (t + 1)])
+            else:
+                wrote["own%d" % (t + 1)] = wrote[fs[1]]
+
+        def signs():
+            if top < L:
+                ts(T.bu[:, top:L], T.cs[:, top:L], T.cols[:, 6:7], 61 * K, A.is_ge, A.mult, ["cs", "c6"], names("bb", top, L))
+
+        def reach(i0, i1, b, pb):
+            d, c1 = int(last and i0 > 0), min(i1, top)
+            ts(T.bu[:, i0:c1], [T.p1, T.p2][d][:, i0:c1], thc, 61 * K, A.is_ge, A.mult, names("cnt", i0, c1) + ["thc"],
+               names("bb", i0, c1), [1 + d])
+            mm(pb[:, i0:i1], T.bo[:], T.bu[:, i0:i1], False, True, names("bb", i0, i1) + ["bo"], names("sj", i0, i1), [b])
+
+        def final(i0, i1, b, pb):
+            m, mn, sb = T.p0[:, L + i0:L + i1], names("mp", i0, i1), names("sb", i0, i1)
+            return [lambda: ts(T.sb[:, i0:i1], T.p3[:, i0:i1], 0.0, None, A.is_gt, None, names("sj", i0, i1), sb, [3]),
+                    lambda: tt(m, T.sb[:, i0:i1], m, A.mult, sb + mn, mn, [0]),
+                    lambda: tt(T.lev[:, i0:i1], T.sb[:, i0:i1], T.p4[:, i0:i1], A.add, sb + ["lv"], names("lev", i0, i1), [4]),
+                    lambda: tt(T.oo[:, i0:i1], m, T.kn[:, i0:i1], A.add, mn + ["kn"], names("oo", i0, i1), [0])]
+
+        between = {}
+        if last:
+            early = final(*parts[0])
+            between = {2: lambda: ts(T.tmp[:], lo, K, None, A.is_lt, None, full("lo"), ["tmp"], [0]),
+                       6: lambda: ts(T.p4[:, 0:L], T.key[:], 1 / K, -0.5 + 0.5 / K, A.mult, A.add, full("key"), ["lv"], [4]),
+                       10: lambda: tt(T.kn[:], T.tmp[:], lo, A.mult, ["tmp"] + full("lo"), ["kn"], [0]),
+                       14: lambda: ts(T.p4[:, 0:L], T.p4[:, 0:L], WHOLE, -WHOLE, A.add, A.add, ["lv"], ["lv"], [4]),
+                       18: lambda: tt(mp, cc, T.kn[:], A.subtract, ["cc", "kn"], full("mp"), [0, 7]),
+                       -10: lambda: reach(*parts[0]), -5: early[0], -4: lambda: limit(*parts[1]), -2: early[1], -1: early[2]}
+        calls = [(c0, c1, k) for c0, c1 in pairs(COMPARE[t]) for k in range(16)]
+        for n, (c0, c1, k) in enumerate(calls):
+            for at in (n, n - len(calls)):
+                if at in between:
+                    between[at]()
+            b = int(last and c0 >= cut)
+            ck = ["cmp%d_%d" % (k, c0)]
+            tt(T.cmp[:, L * k + c0:L * k + c1], T.gat[:, 16 * c0 + k:16 * c1:16], T.p0[:, c0:c1], A.is_ge,
+               names("ga", c0, c1) + names("lo", c0, c1), ck, [0])
+            mm([T.p1, T.p2][b][:, c0:c1], T.eye[:], T.cmp[:, L * k + c0:L * k + c1], k == 0, k == 15,
+               ck + ["eye"], names("cnt", c0, c1), [1 + b], k == 15)
+        if last:
+            early[3]()
+            signs()
+            reach(*parts[1])
+            for step_ in final(*parts[1]):
+                step_()
+            dma("a", T.yr[:, L * t:L * t + L], T.lev[0:128:16, :], full("lev"), [])
+            dma("s", T.yo[:], T.oo[:], full("oo"), [])
+            break
+        if t == 0:
+            ts(mp, T.tmp[:], 0.0, K - 4096, A.is_gt, A.mult, ["tmp"], full("mp"), [0])
+            tt(T.kn[:], u1, cc, A.add, ["u1", "cc"], ["kn"], [7])
+        else:
+            tt(u1, T.key[:], lo, A.add, full("key") + full("lo"), ["u1"], [0])
+            signs()
+        for part in parts:
+            reach(*part)
+        for p in range(16):
+            mm(sl, T.zs[:, 15 - p:143 - p], T.bu[:, p:2 * L:16], False, p == 15, full("bb") + ["u1", "zs"], ["sl"], [4], p == 15)
+        fown, fn = slots(T.ft, M * t)(r), ["fown%d_0" % t, "fown%d_1" % t]
+        if t == 0:
+            tt(T.key[:], mp, T.tmp[:], A.add, full("mp") + ["tmp"], full("key"), [0])
+        else:
+            tt(T.kn[:], u1, cc, A.add, ["u1", "cc"], ["kn"], [7])
+        for i0, i1, b, pb in parts:
+            tt(T.p0[:, L + i0:L + i1], pb[:, i0:i1], T.kn[:, i0:i1], A.min, names("sj", i0, i1) + ["kn"], names("mp", i0, i1), [0, b])
+        for n, (i0, i1, b, pb) in enumerate(parts):
+            tt(T.ft[:, M * t + L * r + i0:M * t + L * r + i1], T.p0[:, L + i0:L + i1], T.key[:, i0:i1], A.max,
+               names("mp", i0, i1) + names("key", i0, i1), [fn[n]], [0])
+            act(T.sb[:, i0:i1], pb[:, i0:i1], F.Sign, 0.0, 1.0, names("sj", i0, i1), names("sb", i0, i1), [b])
+        spread(fown, slots(T.ft, M * t), fn, "ffar%d" % t)
+        act(T.ks[:], fown, F.Copy, 0.0, 1.0, fn, ["ks"])
+        if t + 2 < RO:
+            make_cc(t + 1)
+        else:
+            act(cc, T.m1[:], F.Relu, M * RO - BIG, 1.0, ["m1"], ["cc"], [7])
+        ts(T.ua[:, 0:16], T.p4[:, 0:16], bc, 16 * K, A.is_ge, A.mult, ["sl", "bc"] + ["bs%d" % n for n in range(3)], ["u1a"], [4])
+        cp(T.ua[:, 16:32], T.p4[:, 16:32], ["sl"], ["u1b"], [4])
+        tt(T.ua[:, 32:48], T.p4[:, 0:16], T.ua[:, 0:16], A.add, ["sl", "u1a"], ["u2"], [4])
+        tt(T.ui[:, 0:16], T.ua[:, 32:48], T.ua[:, 16:32], A.add, ["u1b", "u2"], ["u4"])
+        ts(T.ui[:, 16:32], T.ui[:, 0:16], 14, M - 1, A.arith_shift_right, A.bitwise_and, ["u4"], ["u5"])
+        cp(T.ol[:], T.ui[:, 16:32], ["u5"], ["ol"])
+        mm(rr, T.et[:, 0:8], u1, True, False, ["et0", "u1"], ["rr"], [5], False)
+        mm(rr, T.et[:, 8:16], T.sb[:], False, True, ["et1"] + full("sb"), ["rr"], [5])
     for s in total:
         wait("g", (s, total[s]))

@@ -3,25 +3,27 @@ from concourse.mybir import AluOpType, ActivationFunctionType
 
 L, M, RO = 256, 2048, 4
 K = 16384.0
+C = 128 * K
 BIG = 65536.0
+FAR = 4194304.0
 WHOLE = 12582912.0
-HEAD = 64
-GATHER = [[0, 64, 128, 192, 232]] + 3 * [[0, 64, 128, 176]]
-SHARE = [[232, 256]] + 3 * [[176, 256]]
-COMPARE = [[0, 64, 128, 192, 256]] + 2 * [[0, 96, 224]] + [[0, 96, 160, 224]]
+HEADS = [0, 64, 128, L]
+GATHER = [[0, 64, 128, 192, 224]] + 3 * [[0, 64, 128, 184]]
+SHARE = [[224, 232, 240, 256]] + 3 * [[184, 248, 256]]
+COMPARE = [[0, 64, 128, 192, 256]] + 3 * [[0, 128, 224]]
 HALF = 128
 
 SCRATCH = {"p%d" % b: ("psum", [128, 512], "float32") for b in range(8)}
 for dtype, tiles in (
         ("float32", dict(tab=4 * M + L, ft=3 * M, gat=16 * L, zero=3 * L, cols=8, base=96, ys=L, ks=L, ua=48, tmp=L, kn=L,
-                         ox=L, oo=L, eyef=128, m1=L, m2=L, lev=L, nl=L, cs=L)),
-        ("bfloat16", dict(cmp=16 * L, signs=16 * 64, ones=L, eye=128, bo=128, zs=144, et=16, bu=2 * L, lim=L, sb=L)),
-        ("int32", dict(coli=L, omi=L, pi=8, zi=L, ui=32, key=L, qi=L)),
-        ("uint16", dict(off=L, ol=16))):
+                         ox=L, oo=L, eyef=256, m1=L, m2=L, lev=L, nl=L, cs=L, key=L)),
+        ("bfloat16", dict(cmp=16 * L, signs=16 * 64, ones=L, eye=128, bo=256, zs=144, et=16, bu=2 * L, lim=2 * L, sb=L, one=L)),
+        ("int32", dict(coli=L, omi=L, pi=8, zi=L, ui=80, qi=L)),
+        ("uint16", dict(off=L, ol=32))):
     SCRATCH.update({name: ("sbuf", [128, n], dtype) for name, n in tiles.items()})
 SCRATCH.update({"mti": ("sbuf", [8, 264], "int32"), "mtb": ("sbuf", [8, 264], "bfloat16"),
                 "e1": ("sbuf", [8, 128], "bfloat16"), "ey": ("sbuf", [8, 272], "bfloat16"),
-                "orr": ("sbuf", [8, 3 * L], "float32")})
+                "orr": ("sbuf", [8, RO * L], "float32")})
 SEMAPHORES = (["qv", "qa", "qt", "qg", "sent"] + ["arr%d" % k for k in range(7)] + ["via%d" % k for k in range(7)]
               + ["dma%d" % k for k in range(9)])
 
@@ -140,8 +142,8 @@ def rank_program(g, core, T, topo):
     def slots(buf, c0):
         return lambda q: buf[:, c0 + L * q:c0 + L * (q + 1)]
 
-    lo, mp, sj, sl, rr = T.p0[:, 0:L], T.p0[:, L:2 * L], T.p3[:, 0:L], T.p4[:, 0:32], T.p5[0:8, 0:L]
-    step, shift, cc, bb, u1 = T.p6[:, 0:L], T.p6[:, L:2 * L], T.p7[:, 0:L], T.bu[:, 0:L], T.bu[:, L:2 * L]
+    mp, sl, rr, more = T.p1[:, L:2 * L], T.p4[:, 0:32], T.p6[0:8, L:2 * L], T.p5[:, 0:L]
+    step, shift, cc, bb, u1 = T.p6[:, 0:L], T.p7[:, L:2 * L], T.p7[:, 0:L], T.bu[:, 0:L], T.bu[:, L:2 * L]
     thc, bc, jc, j5 = T.cols[:, 0:1], T.cols[:, 1:2], T.cols[:, 2:3], T.cols[:, 3:4]
 
     def make_cc(t):
@@ -157,71 +159,86 @@ def rank_program(g, core, T, topo):
     op("g", lambda: g.affine_select(T.e1[:], T.ones[0:8, 0:128], [[1, 128]], A.is_ge, 0.0, 0, -16), ["ones"], ["e1"])
     op("g", lambda: g.affine_select(T.ey[:, 128:272], T.ones[0:8, 0:144], [[1, 144]], A.is_equal, 0.0, -15, -16), ["ones"], ["ey1"])
     op("g", lambda: g.affine_select(T.ey[:, 0:128], T.e1[:], [[-1, 128]], A.is_ge, 0.0, 15, 16), ["e1"], ["ey0"])
-    fill(u1, K, ["u1"])
+    fill(u1, C + K, full("u1"))
     ts(T.pi[:, 4:5], T.pi[:, 0:1], 15, None, A.bitwise_and, None, ["pi"], ["pj"])
     fill(T.base[:], 0.0, ["bs"])
     ts(j5, T.pi[:, 4:5], 5.0, None, A.mult, None, ["pj"], ["j5"])
     cp(jc, T.pi[:, 4:5], ["pj"], ["jc"])
-    ts(T.cols[:, 4:5], T.pi[:, 4:5], 5.0, -16.0, A.mult, A.add, ["pj"], ["c4"])
+    ts(T.cols[:, 4:5], T.pi[:, 4:5], 5.0, 8 * 61 - 16 * (C / K + 1), A.mult, A.add, ["pj"], ["c4"])
     ts(T.ui[:, 0:16], T.ua[:, 0:16], j5, -77.0, A.add, A.add, ["base", "j5"], ["u4"])
     for t in range(RO - 1):
         ts(T.base[:, 32 * t + 16:32 * t + 32], T.ua[:, 16 * t:16 * t + 16], T.cols[:, 4:5], K, A.add, A.mult,
            ["base", "c4", "bs"], ["bs%d" % t])
     ts(T.ui[:, 16:32], T.ui[:, 0:16], M - 1, None, A.bitwise_and, None, ["u4"], ["u5"])
     mine = slots(T.tab, 0)(r)
-    ts(mp, T.omi[:], 1.0 / 8192, None, A.mult, None, ["om"], full("mp"), [0])
-    cp(T.ol[:], T.ui[:, 16:32], ["u5"], ["ol"])
-    tt(mine, T.coli[:], mp, A.add, ["col"] + full("mp"), ["own0"], [0])
+    ts(mp, T.omi[:], 1.0 / 8192, None, A.mult, None, ["om"], full("mp"), [1])
+    cp(T.ol[:, 0:16], T.ui[:, 16:32], ["u5"], ["ol"])
+    tt(mine, T.coli[:], mp, A.add, ["col"] + full("mp"), ["own0"], [1])
     op("g", lambda: g.iota(T.lev[:], [[1, L]], int(BIG) + L * r, 0, allow_small_or_imprecise_dtypes=True), [], ["lev"])
     spread(mine, slots(T.tab, 0), ["own0"], "far0")
 
     op("g", lambda: g.affine_select(T.eye[:], T.ones[:, 0:128], [[-1, 128]], A.is_equal, 0.0, 0, 1), ["ones"], ["eye"])
     cp(T.mtb[:, 0:L + 1], T.mti[:, 0:L + 1], ["mem", "th"], ["mtb"])
-    mm(T.p1[:, 0:272], T.ey[:, 0:128], T.ey[:], True, True, ["ey0", "ey1"], ["blk"], [1])
+    mm(T.p2[:, 0:272], T.ey[:, 0:128], T.ey[:], True, True, ["ey0", "ey1"], ["blk"], [2])
     mm(T.p3[:, 0:L + 1], T.ey[:, 0:128], T.mtb[:, 0:L + 1], True, True, ["ey0", "mtb"], ["mt"], [3])
     act(T.m1[:], T.lev[:], F.Identity, 0.0, 1.0 / M, ["lev"], ["m1"])
     act(T.m2[:], T.lev[:], F.Identity, 2 * BIG / M, -1.0 / M, ["lev"], ["m2"])
-    act(T.bo[:], T.p1[:, 0:128], F.Copy, 0.0, 16.0, ["blk"], ["bo"], [1])
-    act(T.zs[:], T.p1[:, 128:272], F.Copy, 0.0, 1.0, ["blk"], ["zs"], [1])
+    act(T.bo[:, 0:128], T.p2[:, 0:128], F.Copy, 0.0, FAR, ["blk"], ["bo"], [2])
+    act(T.zs[:], T.p2[:, 128:272], F.Copy, 0.0, 1.0, ["blk"], ["zs"], [2])
     for n, wgt in enumerate([1.0 / (16 * K), 1.0 / 32]):
-        act(T.et[:, 8 * n:8 * n + 8], T.p1[:, 0:128:16], F.Copy, 0.0, wgt, ["blk"], ["et%d" % n], [1])
+        act(T.et[:, 8 * n:8 * n + 8], T.p2[:, 0:128:16], F.Copy, 0.0, wgt, ["blk"], ["et%d" % n], [2])
     ts(T.zi[:], T.omi[:], -1.0, None, A.mult, None, ["om"], ["zi"])
     ts(step, T.p3[:, 0:L], jc, float(M), A.is_equal, A.mult, ["mt", "jc"], ["step"], [3, 6])
     ts(T.qi[:], T.zi[:], 4095, None, A.bitwise_and, None, ["zi"], full("qi"))
     tt(T.m1[:], T.m1[:], step, A.mult, ["m1", "step"], ["m1"], [6])
     cp(thc, T.p3[:, L:L + 1], ["mt"], ["thc"], [3])
     act(cc, T.m1[:], F.Relu, M - L * r - BIG, 1.0, ["m1"], ["cc"], [7])
-    cp(mp, T.qi[:], full("qi"), full("mp"), [0])
+    cp(mp, T.qi[:], full("qi"), full("mp"), [1])
     tt(T.m2[:], T.m2[:], step, A.mult, ["m2", "step"], ["m2"], [6])
-    ts(shift, T.p3[:, 0:L], jc, float(L * r), A.is_equal, A.mult, ["mt", "jc"], ["shift"], [3, 6])
-    ts(T.cols[:, 5:6], thc, -0.5, -16 * 61 * K, A.add, A.mult, ["thc"], ["c5"])
-    ts(bc, thc, 61 * K, None, A.mult, None, ["thc"], ["bc"])
-    ts(T.cols[:, 6:7], thc, 2.0, -16.0, A.mult, A.add, ["thc"], ["c6"])
+    ts(shift, T.p3[:, 0:L], jc, float(L * r), A.is_equal, A.mult, ["mt", "jc"], ["shift"], [3, 7])
+    ts(T.cols[:, 5:6], thc, -2 * FAR, 17 * FAR, A.mult, A.add, ["thc"], ["c5"])
+    ts(bc, thc, 2.0, -16.0, A.mult, A.add, ["thc"], ["bc"])
+    ts(T.cols[:, 6:7], thc, -2.0, 17.0, A.mult, A.add, ["thc"], ["c6"])
+    ts(T.cols[:, 7:8], thc, -1.0, 0.5, A.mult, A.add, ["thc"], ["c7"])
     tt(T.ys[:], mine, cc, A.max, ["own0", "cc"], ["ys"], [7])
-    act(T.lim[:], T.ones[:], F.Identity, 0.0, T.cols[:, 5:6], ["ones", "c5"], ["lim"])
-    act(T.eyef[:], T.eye[:], F.Copy, 0.0, 1.0, ["eye"], ["eyef"])
+    act(T.one[:], step, F.Copy, 0.0, 1.0, ["step"], ["one"], [6])
+    act(T.lim[:, 0:L], T.ones[:], F.Identity, 0.0, T.cols[:, 5:6], ["ones", "c5"], ["lim"])
     make_cc(0)
+    act(T.bo[:, 128:256], T.bo[:, 0:128], F.Copy, 0.0, -1.0, ["bo"], ["nbo"])
+    act(T.lim[:, L:2 * L], T.lim[:, 0:L], F.Copy, 0.0, -1.0, ["lim"], ["nlim"])
+    act(T.eyef[:, 0:128], T.eye[:], F.Copy, 0.0, 1.0, ["eye"], ["eyef"])
+    act(T.eyef[:, 128:256], T.eye[:], F.Copy, 0.0, -1.0, ["eye"], ["negf"])
 
     for t in range(RO):
         last = t == RO - 1
         e0 = M * (t + 1)
         par = T.tab[:, M * t:e0]
         tabs = ["own%d" % s for s in range(t + 1)] + ["far%d" % s for s in range(t + 1)] + ["zero%d" % s for s in range(1, t + 1)]
-        y, fs = T.tab[:, e0:e0 + L], ["y%d_0" % t, "y%d_1" % t]
-        heads = ((0, 0, HEAD), (1, HEAD, L))
-        for h, i0, i1 in heads:
+        heads = pairs(HEADS)
+        y, fs = T.tab[:, e0:e0 + L], ["y%d_%d" % (t, h) for h in range(len(heads))]
+
+        def vector(h):
+            i0, i1 = heads[h]
             tt(T.tab[:, e0 + i0:e0 + i1], par.indirect(T.ol[:, i0 // 16:i1 // 16]), T.ys[:, i0:i1], A.max,
                tabs[t::t + 1][:2] + tabs[-1:] + ["ol", "ys"], [fs[h]])
-        for h, i0, i1 in heads:
+
+        def offsets(h):
+            i0, i1 = heads[h]
             cp(T.off[:, i0:i1], T.tab[:, e0 + i0:e0 + i1], [fs[h]], ["off%d" % h])
             for c0, c1 in pairs(GATHER[t]):
                 if i0 <= c0 < i1:
                     act(T.gat[:, 16 * c0:16 * c1], T.tab[:, 0:e0 + i1].indirect(T.off[:, c0:c1]), F.Copy, 0.0, 1.0,
                         tabs + fs[:h + 1] + ["off%d" % h], names("ga", c0, c1))
-            if t == 0 and h == 0:
-                ts(T.key[:], par.indirect(T.ol[:]), -8192.0, None, A.mult, None, ["own0", "far0", "ol"], full("key"))
+
+        vector(0)
+        for h in range(1, len(heads)):
+            vector(h)
+            offsets(h - 1)
         if t == 0:
-            ts(T.qi[:], T.key[:], 4095, None, A.bitwise_and, None, full("key"), full("qi"))
+            ts(T.zi[:], par.indirect(T.ol[:, 0:16]), -8192.0, None, A.mult, None, ["own0", "far0", "ol"], ["zi"])
+        offsets(len(heads) - 1)
+        if t == 0:
+            ts(T.qi[:], T.zi[:], 4095, None, A.bitwise_and, None, ["zi"], full("qi"))
 
         def slot(q):
             return slots(T.zero, L * t)(0) if q == 0 else slots(T.tab, e0)(q)
@@ -229,146 +246,165 @@ def rank_program(g, core, T, topo):
         def share(n):
             if n < len(SHARE[t]) - 1:
                 c0, c1 = SHARE[t][n:n + 2]
-                cp(T.gat[:, 16 * c0:16 * c1], T.tab[:, 0:e0 + L].indirect(T.off[:, c0:c1]), tabs + fs + ["off1"], names("ga", c0, c1))
+                cp(T.gat[:, 16 * c0:16 * c1], T.tab[:, 0:e0 + L].indirect(T.off[:, c0:c1]), tabs + fs + ["off%d" % (len(heads) - 1)],
+                   names("ga", c0, c1))
 
         def onward():
             if not last:
-                tt(T.ys[:], y, step, A.add, fs + ["step"], ["ys"], [6])
+                mm(more, T.eyef[:, 0:128], y, True, False, fs + ["eyef"], ["more"], [5], False)
+                mm(more, T.eye[:], T.one[:], False, True, ["eye", "one"], ["more"], [5])
 
-        if last:
-            tt(T.ox[:], y, shift, A.add, fs + ["shift"], ["ox"], [6])
-        elif r == 0:
-            spread(y, slot, fs, "far%d" % (t + 1))
-        else:
-            tt(slot(r), y, shift, A.add, fs + ["shift"], ["own%d" % (t + 1)], [6])
-            spread(slot(r), slot, ["own%d" % (t + 1)], "far%d" % (t + 1))
+        def vectors():
+            if last:
+                tt(T.ox[:], y, shift, A.add, fs + ["shift"], ["ox"], [7])
+            elif r == 0:
+                spread(y, slot, fs, "far%d" % (t + 1))
+            else:
+                tt(slot(r), y, shift, A.add, fs + ["shift"], ["own%d" % (t + 1)], [7])
+                spread(slot(r), slot, ["own%d" % (t + 1)], "far%d" % (t + 1))
+
+        if t > 0:
+            vectors()
         top = COMPARE[t][-1]
-        cut = COMPARE[t][-2] if last else HALF
-        parts = [(0, cut, 3, T.p3), (cut, L, 3, T.p3) if last else (cut, L, 2, T.p2)]
-
-        def limit(i0, i1, b, pb):
+        parts = [(0, HALF, 3, T.p3, 4, T.p4), (HALF, L, 2, T.p2, 7, T.p7)]
+        for i0, i1, b, pb, d, pd in parts:
             mm(pb[:, i0:i1], T.eye[:], T.lim[:, i0:i1], True, False, ["eye", "lim"], names("sj", i0, i1), [b], False)
-
-        for part in parts[:1] if last else parts:
-            limit(*part)
+            if last:
+                mm(pd[:, i0:i1], T.eye[:], T.lim[:, L + i0:L + i1], True, False, ["eye", "nlim"], names("nj", i0, i1), [d], False)
         if not last:
-            mm(sl, T.eyef[:], T.base[:, 32 * t:32 * t + 32], True, False, ["eyef", "bs%d" % t], ["sl"], [4], False)
+            mm(sl, T.eyef[:, 0:128], T.base[:, 32 * t:32 * t + 32], True, False, ["eyef", "bs%d" % t], ["sl"], [4], False)
+        marks = [(0, HALF, 0, T.p0), (HALF, L, 6, T.p6)]
+        counts = [(1, T.p1), (0, T.p0)]
+
+        def level(n):
+            act(T.orr[:, L * n:L * n + L], rr, F.Identity, -0.5 - C / K, 1.0, ["rr"], ["orr%d" % n], [6])
+
+        def lanes():
+            ts(T.nl[:, top:L], T.p6[:, top:L], -1.0, 0.5, A.mult, A.add, names("lo", top, L), ["nl"], [6])
+            for i in range(top, L):
+                op("a", lambda: S.activation(T.signs[:, 16 * (i - top):16 * (i - top + 1)], T.gat[:, 16 * i:16 * i + 16], F.Sign,
+                                             bias=T.nl[:, i:i + 1], scale=1.0, accum_out=T.cs[:, i:i + 1]),
+                   names("ga", top, L) + ["nl"], ["cs"] if i == L - 1 else [], (), i == L - 1)
+
         if t == 0:
-            tt(T.tmp[:], T.qi[:], mp, A.max, full("qi") + full("mp"), ["tmp"], [0])
             share(0)
-            ts(lo, T.tmp[:], -1.0, 4096.0, A.mult, A.add, ["tmp"], full("lo"), [0])
+            tt(T.tmp[:], T.qi[:], mp, A.max, full("qi") + full("mp"), ["tmp"], [1])
+            share(1)
+            for i0, i1, b, pb in marks:
+                ts(pb[:, i0:i1], T.tmp[:, i0:i1], -1.0, 4096.0, A.mult, A.add, ["tmp"], names("lo", i0, i1), [b])
+            vectors()
             onward()
+            act(T.key[:], T.tmp[:], F.Identity, C, 1.0, ["tmp"], full("key"))
         else:
             onward()
             share(0)
-            two = pairs([0, COMPARE[t][1], L])
-            for i0, i1 in two:
+            if last:
+                mm(more, T.eye[:], T.lim[:, 0:L], True, False, ["eye", "lim"], ["more"], [5], False)
+                ts(T.ox[:], T.ox[:], WHOLE, -WHOLE, A.add, A.add, ["ox"], ["ox"])
+            for i0, i1, b, pb in marks:
                 tt(T.key[:, i0:i1], T.ft[:, M * (t - 1):M * t].indirect(T.ol[:, i0 // 16:i1 // 16]), T.ks[:, i0:i1], A.max,
                    ["fown%d_0" % (t - 1), "fown%d_1" % (t - 1), "ffar%d" % (t - 1), "ks", "ol"], names("key", i0, i1))
-            for i0, i1 in two:
-                ts(T.qi[:, i0:i1], T.key[:, i0:i1], int(K) - 1, None, A.bitwise_and, None, names("key", i0, i1), names("qi", i0, i1))
-            ts(T.p0[:, 0:two[0][1]], T.qi[:, 0:two[0][1]], -1.0, K, A.mult, A.add, names("qi", *two[0]), names("lo", *two[0]), [0])
-            if top < L:
-                ts(T.nl[:, top:L], T.qi[:, top:L], 0.5 - K, None, A.add, None, names("qi", top, L), ["nl"])
-            ts(T.p0[:, two[0][1]:L], T.qi[:, two[0][1]:L], -1.0, K, A.mult, A.add, names("qi", *two[1]), names("lo", *two[1]), [0])
-        for i in range(top, L):
-            op("a", lambda: S.activation(T.signs[:, 16 * (i - top):16 * (i - top + 1)], T.gat[:, 16 * i:16 * i + 16], F.Sign,
-                                         bias=T.nl[:, i:i + 1], scale=1.0, accum_out=T.cs[:, i:i + 1]),
-               names("ga", top, L) + ["nl"], ["cs"] if i == L - 1 else [], (), i == L - 1)
-        if last:
-            act(T.ys[:], T.ox[:], F.Identity, WHOLE, 1.0, ["ox"], ["ys"])
-            act(T.orr[:, L * t - L:L * t], rr, F.Identity, -0.5, 1.0, ["rr"], ["orr"], [5])
-            act(T.ox[:], T.ys[:], F.Identity, -WHOLE, 1.0, ["ys"], ["ox"])
-            dma("s", T.yr[:, 0:L * t], T.orr[:], ["orr"], [])
-            dma("s", T.yx[:], T.ox[:], ["ox"], [])
-        else:
-            if t > 0:
-                act(T.orr[:, L * t - L:L * t], rr, F.Identity, -0.5, 1.0, ["rr"], ["orr"], [5])
+            for i0, i1, b, pb in marks:
+                mm(pb[:, i0:i1], T.eyef[:, 128:256], T.key[:, i0:i1], True, False, names("key", i0, i1) + ["negf"],
+                   names("lo", i0, i1), [b], False)
+                ts(T.bu[:, L + i0:L + i1], T.key[:, i0:i1], K / 2 + 0.5, None, A.add, None, names("key", i0, i1), names("u1", i0, i1))
+                mm(pb[:, i0:i1], T.eye[:], T.bu[:, L + i0:L + i1], False, True, names("u1", i0, i1) + ["eye"], names("lo", i0, i1), [b])
+
+            share(1)
+            if last:
+                dma("s", T.yx[:], T.ox[:], ["ox"] + full("key"), [])
+                dma("s", T.yr[:, 0:L * t], T.orr[:, 0:L * t], ["orr%d" % n for n in range(t)], [])
+
+        def known(i0, i1, b, pb):
+            ts(T.tmp[:, i0:i1], pb[:, i0:i1], K, None, A.is_lt, None, names("lo", i0, i1), names("tm", i0, i1), [b])
+
+        def kept(i0, i1, b, pb):
+            tt(T.kn[:, i0:i1], T.tmp[:, i0:i1], pb[:, i0:i1], A.mult, names("tm", i0, i1) + names("lo", i0, i1), names("kn", i0, i1), [b])
+
+        def settle():
             if r > 0:
                 act(y, slot(0), F.Copy, 0.0, 1.0, ["far%d" % (t + 1)], fs + ["zero%d" % (t + 1)])
             else:
-                wrote["own%d" % (t + 1)] = wrote[fs[1]]
+                wrote["own%d" % (t + 1)] = wrote[fs[-1]]
 
-        def signs():
-            if top < L:
-                ts(T.bu[:, top:L], T.cs[:, top:L], T.cols[:, 6:7], 61 * K, A.is_ge, A.mult, ["cs", "c6"], names("bb", top, L))
+        def reach(i0, i1, b, pb, d, pd):
+            c1, (e, pe) = min(i1, top), counts[i0 >= HALF]
+            act(T.bu[:, i0:c1], pe[:, i0:c1], F.Sign, T.cols[:, 7:8], 1.0, names("cnt", i0, c1) + ["c7"], names("bb", i0, c1), [e])
+            mm(pb[:, i0:i1], T.bo[:, 0:128], T.bu[:, i0:i1], False, True, names("bb", i0, i1) + ["bo"], names("sj", i0, i1), [b])
+            if last:
+                mm(pd[:, i0:i1], T.bo[:, 128:256], T.bu[:, i0:i1], False, True, names("bb", i0, i1) + ["nbo"], names("nj", i0, i1), [d])
 
-        def reach(i0, i1, b, pb):
-            d, c1 = int(last and i0 > 0), min(i1, top)
-            ts(T.bu[:, i0:c1], [T.p1, T.p2][d][:, i0:c1], thc, 61 * K, A.is_ge, A.mult, names("cnt", i0, c1) + ["thc"],
-               names("bb", i0, c1), [1 + d])
-            mm(pb[:, i0:i1], T.bo[:], T.bu[:, i0:i1], False, True, names("bb", i0, i1) + ["bo"], names("sj", i0, i1), [b])
-
-        def final(i0, i1, b, pb):
-            m, mn, sb = T.p0[:, L + i0:L + i1], names("mp", i0, i1), names("sb", i0, i1)
-            return [lambda: ts(T.sb[:, i0:i1], T.p3[:, i0:i1], 0.0, None, A.is_gt, None, names("sj", i0, i1), sb, [3]),
-                    lambda: tt(m, T.sb[:, i0:i1], m, A.mult, sb + mn, mn, [0]),
-                    lambda: tt(T.lev[:, i0:i1], T.sb[:, i0:i1], T.p4[:, i0:i1], A.add, sb + ["lv"], names("lev", i0, i1), [4]),
-                    lambda: tt(T.oo[:, i0:i1], m, T.kn[:, i0:i1], A.add, mn + ["kn"], names("oo", i0, i1), [0])]
-
-        between = {}
+        for n, (c0, c1) in enumerate(pairs(COMPARE[t])):
+            if n > 0 and t == 0:
+                share(n + 1)
+            b, pb = marks[c0 >= HALF][2:]
+            for k in range(16):
+                if top < L and (n, k) == (0, 3):
+                    lanes()
+                ck = ["cmp%d_%d" % (k, c0)]
+                tt(T.cmp[:, L * k + c0:L * k + c1], T.gat[:, 16 * c0 + k:16 * c1:16], pb[:, c0:c1], A.is_ge,
+                   names("ga", c0, c1) + names("lo", c0, c1), ck, [b])
+                mm(counts[c0 >= HALF][1][:, c0:c1], T.eye[:], T.cmp[:, L * k + c0:L * k + c1], k == 0, k == 15,
+                   ck + ["eye"], names("cnt", c0, c1), [counts[c0 >= HALF][0]], k == 15)
+                if last and (c1, k) == (HALF, 12):
+                    known(*marks[0])
+                if last and (c1, k) == (HALF, 14):
+                    kept(*marks[0])
+        if t == 0:
+            ts(T.p6[:, L:2 * L], T.tmp[:], 0.0, K - 4096, A.is_gt, A.mult, ["tmp"], ["has"], [6])
+        if not last:
+            tt(T.kn[:], u1, cc, A.add, full("u1") + ["cc"], full("kn"), [7])
+        if t == 0:
+            tt(T.key[:], T.p6[:, L:2 * L], T.key[:], A.add, ["has"] + full("key"), full("key"), [6])
         if last:
-            early = final(*parts[0])
-            between = {2: lambda: ts(T.tmp[:], lo, K, None, A.is_lt, None, full("lo"), ["tmp"], [0]),
-                       6: lambda: ts(T.p4[:, 0:L], T.key[:], 1 / K, -0.5 + 0.5 / K, A.mult, A.add, full("key"), ["lv"], [4]),
-                       10: lambda: tt(T.kn[:], T.tmp[:], lo, A.mult, ["tmp"] + full("lo"), ["kn"], [0]),
-                       14: lambda: ts(T.p4[:, 0:L], T.p4[:, 0:L], WHOLE, -WHOLE, A.add, A.add, ["lv"], ["lv"], [4]),
-                       18: lambda: tt(mp, cc, T.kn[:], A.subtract, ["cc", "kn"], full("mp"), [0, 7]),
-                       -10: lambda: reach(*parts[0]), -5: early[0], -4: lambda: limit(*parts[1]), -2: early[1], -1: early[2]}
-        calls = [(c0, c1, k) for c0, c1 in pairs(COMPARE[t]) for k in range(16)]
-        for n, (c0, c1, k) in enumerate(calls):
-            for at in (n, n - len(calls)):
-                if at in between:
-                    between[at]()
-            b = int(last and c0 >= cut)
-            ck = ["cmp%d_%d" % (k, c0)]
-            tt(T.cmp[:, L * k + c0:L * k + c1], T.gat[:, 16 * c0 + k:16 * c1:16], T.p0[:, c0:c1], A.is_ge,
-               names("ga", c0, c1) + names("lo", c0, c1), ck, [0])
-            mm([T.p1, T.p2][b][:, c0:c1], T.eye[:], T.cmp[:, L * k + c0:L * k + c1], k == 0, k == 15,
-               ck + ["eye"], names("cnt", c0, c1), [1 + b], k == 15)
+            known(*marks[1])
+            kept(*marks[1])
+        reach(*parts[0])
+        if top < L:
+            act(T.bu[:, top:L], T.cs[:, top:L], F.Sign, T.cols[:, 6:7], 1.0, ["cs", "c6"], names("bb", top, L))
+        reach(*parts[1])
         if last:
-            early[3]()
-            signs()
-            reach(*parts[1])
-            for step_ in final(*parts[1]):
-                step_()
-            dma("a", T.yr[:, L * t:L * t + L], T.lev[0:128:16, :], full("lev"), [])
+            mm(more, T.bo[:, 0:128], bb, False, True, full("bb") + ["bo"], ["more"], [5])
+            mm(rr, T.et[:, 0:8], u1, True, False, ["et0"] + full("u1"), ["rr"], [6], False)
+            act(T.sb[:], more, F.Sign, 0.0, 1.0, ["more"], full("sb"), [5])
+            mm(rr, T.et[:, 8:16], T.sb[:], False, True, ["et1"] + full("sb"), ["rr"], [6])
+            level(t)
+            dma("a", T.yr[:, L * t:L * t + L], T.orr[:, L * t:L * t + L], ["orr%d" % t], [])
+            for i0, i1, b, pb, d, pd in parts:
+                tt(T.p1[:, L + i0:L + i1], pb[:, i0:i1], T.lev[:, i0:i1], A.min, names("sj", i0, i1) + ["lev"], names("mp", i0, i1), [1, b])
+                tt(T.tmp[:, i0:i1], pd[:, i0:i1], T.kn[:, i0:i1], A.min, names("nj", i0, i1) + names("kn", i0, i1), names("tm", i0, i1), [d])
+            for i0, i1, b, pb, d, pd in parts:
+                tt(T.oo[:, i0:i1], T.p1[:, L + i0:L + i1], T.tmp[:, i0:i1], A.max, names("mp", i0, i1) + names("tm", i0, i1),
+                   names("oo", i0, i1), [1])
             dma("s", T.yo[:], T.oo[:], full("oo"), [])
             break
-        if t == 0:
-            ts(mp, T.tmp[:], 0.0, K - 4096, A.is_gt, A.mult, ["tmp"], full("mp"), [0])
-            tt(T.kn[:], u1, cc, A.add, ["u1", "cc"], ["kn"], [7])
-        else:
-            tt(u1, T.key[:], lo, A.add, full("key") + full("lo"), ["u1"], [0])
-            signs()
-        for part in parts:
-            reach(*part)
         for p in range(16):
-            mm(sl, T.zs[:, 15 - p:143 - p], T.bu[:, p:2 * L:16], False, p == 15, full("bb") + ["u1", "zs"], ["sl"], [4], p == 15)
+            mm(sl, T.zs[:, 15 - p:143 - p], T.bu[:, p:2 * L:16], False, p == 15, full("bb") + full("u1") + ["zs"], ["sl"], [4],
+               p == 15)
         fown, fn = slots(T.ft, M * t)(r), ["fown%d_0" % t, "fown%d_1" % t]
-        if t == 0:
-            tt(T.key[:], mp, T.tmp[:], A.add, full("mp") + ["tmp"], full("key"), [0])
-        else:
-            tt(T.kn[:], u1, cc, A.add, ["u1", "cc"], ["kn"], [7])
-        for i0, i1, b, pb in parts:
-            tt(T.p0[:, L + i0:L + i1], pb[:, i0:i1], T.kn[:, i0:i1], A.min, names("sj", i0, i1) + ["kn"], names("mp", i0, i1), [0, b])
-        for n, (i0, i1, b, pb) in enumerate(parts):
-            tt(T.ft[:, M * t + L * r + i0:M * t + L * r + i1], T.p0[:, L + i0:L + i1], T.key[:, i0:i1], A.max,
-               names("mp", i0, i1) + names("key", i0, i1), [fn[n]], [0])
+        for n, (i0, i1, b, pb, d, pd) in enumerate(parts):
+            tt(T.p1[:, L + i0:L + i1], pb[:, i0:i1], T.kn[:, i0:i1], A.min, names("sj", i0, i1) + names("kn", i0, i1),
+               names("mp", i0, i1), [1, b])
+        for n, (i0, i1, b, pb, d, pd) in enumerate(parts):
+            tt(T.ft[:, M * t + L * r + i0:M * t + L * r + i1], T.p1[:, L + i0:L + i1], T.key[:, i0:i1], A.max,
+               names("mp", i0, i1) + names("key", i0, i1), [fn[n]], [1])
             act(T.sb[:, i0:i1], pb[:, i0:i1], F.Sign, 0.0, 1.0, names("sj", i0, i1), names("sb", i0, i1), [b])
         spread(fown, slots(T.ft, M * t), fn, "ffar%d" % t)
         act(T.ks[:], fown, F.Copy, 0.0, 1.0, fn, ["ks"])
+        act(T.ys[:], more, F.Copy, 0.0, 1.0, ["more"], ["ys"], [5])
+        settle()
         if t + 2 < RO:
             make_cc(t + 1)
         else:
-            act(cc, T.m1[:], F.Relu, M * RO - BIG, 1.0, ["m1"], ["cc"], [7])
+            act(T.lev[:], T.m1[:], F.Relu, M * RO - BIG, 1.0, ["m1"], ["lev"])
         ts(T.ua[:, 0:16], T.p4[:, 0:16], bc, 16 * K, A.is_ge, A.mult, ["sl", "bc"] + ["bs%d" % n for n in range(3)], ["u1a"], [4])
-        cp(T.ua[:, 16:32], T.p4[:, 16:32], ["sl"], ["u1b"], [4])
-        tt(T.ua[:, 32:48], T.p4[:, 0:16], T.ua[:, 0:16], A.add, ["sl", "u1a"], ["u2"], [4])
+        ts(T.ua[:, 16:32], T.p4[:, 0:16], 30.5 * K, None, A.mult, None, ["sl"], ["u1b"], [4])
+        tt(T.ua[:, 32:48], T.p4[:, 16:32], T.ua[:, 0:16], A.add, ["sl", "u1a"], ["u2"], [4])
         tt(T.ui[:, 0:16], T.ua[:, 32:48], T.ua[:, 16:32], A.add, ["u1b", "u2"], ["u4"])
         ts(T.ui[:, 16:32], T.ui[:, 0:16], 14, M - 1, A.arith_shift_right, A.bitwise_and, ["u4"], ["u5"])
-        cp(T.ol[:], T.ui[:, 16:32], ["u5"], ["ol"])
-        mm(rr, T.et[:, 0:8], u1, True, False, ["et0", "u1"], ["rr"], [5], False)
-        mm(rr, T.et[:, 8:16], T.sb[:], False, True, ["et1"] + full("sb"), ["rr"], [5])
+        cp(T.ol[:, 0:16], T.ui[:, 16:32], ["u5"], ["ol"])
+        mm(rr, T.et[:, 0:8], u1, True, False, ["et0"] + full("u1"), ["rr"], [6], False)
+        mm(rr, T.et[:, 8:16], T.sb[:], False, True, ["et1"] + full("sb"), ["rr"], [6])
+        level(t)
     for s in total:
         wait("g", (s, total[s]))

from concourse.bass import DstId, RemoteDMATransfer
from concourse.mybir import AluOpType, ActivationFunctionType

L, M, RO = 256, 2048, 4
K = 16384.0
C = 128 * K
BIG = 65536.0
FAR = 4194304.0
WHOLE = 12582912.0
HEADS = [0, 64, 128, L]
GATHER = [[0, 64, 128, 192, 224]] + 3 * [[0, 64, 128, 184]]
SHARE = [[224, 232, 240, 256]] + 3 * [[184, 248, 256]]
COMPARE = [[0, 64, 128, 192, 256]] + 3 * [[0, 128, 224]]
HALF = 128

SCRATCH = {"p%d" % b: ("psum", [128, 512], "float32") for b in range(8)}
for dtype, tiles in (
        ("float32", dict(tab=4 * M + L, ft=3 * M, gat=16 * L, zero=3 * L, cols=8, base=96, ys=L, ks=L, ua=48, tmp=L, kn=L,
                         ox=L, oo=L, eyef=256, m1=L, m2=L, lev=L, nl=L, cs=L, key=L)),
        ("bfloat16", dict(cmp=16 * L, signs=16 * 64, ones=L, eye=128, bo=256, zs=144, et=16, bu=2 * L, lim=2 * L, sb=L, one=L)),
        ("int32", dict(coli=L, omi=L, pi=8, zi=L, ui=80, qi=L)),
        ("uint16", dict(off=L, ol=32))):
    SCRATCH.update({name: ("sbuf", [128, n], dtype) for name, n in tiles.items()})
SCRATCH.update({"mti": ("sbuf", [8, 264], "int32"), "mtb": ("sbuf", [8, 264], "bfloat16"),
                "e1": ("sbuf", [8, 128], "bfloat16"), "ey": ("sbuf", [8, 272], "bfloat16"),
                "orr": ("sbuf", [8, RO * L], "float32")})
SEMAPHORES = (["qv", "qa", "qt", "qg", "sent"] + ["arr%d" % k for k in range(7)] + ["via%d" % k for k in range(7)]
              + ["dma%d" % k for k in range(9)])

A = AluOpType
F = ActivationFunctionType


def rank_program(g, core, T, topo):
    r = T.rank_of(core)
    if r is None:
        return
    here = [c for c in T.cores if topo.die(c) == topo.die(core)]
    there = [c for c in T.cores if topo.die(c) != topo.die(core)]
    partner = there[here.index(core)]
    near = [c for c in here if c != core]
    queue = {"v": g.vector, "a": g.scalar, "t": g.tensor, "g": g, "s": g.sync}
    own = {"v": "qv", "a": "qa", "t": "qt", "g": "qg"}
    total, seen, wrote, read, bank = {}, {}, {}, {}, {}
    count = {"dma": 0, "arr": 0}

    def wait(q, tok):
        if seen.get((q, tok[0]), 0) < tok[1]:
            queue[q].wait_ge(T.sem[tok[0]], tok[1])
            seen[(q, tok[0])] = tok[1]

    def order(q, rd, wr, banks):
        need = {}
        toks = [wrote[k] for k in rd + wr + [k + "v" for k in rd] if k in wrote] + [t for k in wr for t in read.get(k, [])]
        toks += [t for b in banks for e, t in bank.get(b, {}).items() if e != q]
        for s, n in toks:
            if not (q == "t" and s == "qt"):
                need[s] = max(need.get(s, 0), n)
        for s in need:
            wait(q, (s, need[s]))

    def note(q, tok, rd, wr, banks):
        for k in rd:
            read.setdefault(k, []).append(tok)
        for k in wr:
            wrote[k] = tok
            read[k] = []
        for b in banks:
            bank.setdefault(b, {})[q] = tok

    def op(q, call, rd, wr, banks=(), inc=True):
        order(q, rd, wr, banks)
        ins = call()
        n = total.get(own[q], 0) + 1
        if inc:
            ins.then_inc(T.sem[own[q]], 1)
            total[own[q]] = n
        note(q, (own[q], n), rd, wr, banks)

    def dma(q, out, in_, rd, wr):
        order(q, rd, wr, ())
        s = "dma%d" % count["dma"]
        count["dma"] += 1
        queue[q].dma_start(out, in_).then_inc(T.sem[s], 16)
        total[s] = 16
        note(q, (s, 16), rd, wr, ())

    eng = [e for e in topo.engines(core, partner) if all(e in topo.engines(core, c) for c in near)]

    def send(cores, sem, src, dst):
        g.remote_dma_fused([RemoteDMATransfer(dst_ids=[DstId(rid=topo.addr(c)[0], pnc=topo.addr(c)[1]) for c in cores],
                                              dma_engine_mask=sum(1 << e for e in eng), remote_sem=T.sem[sem],
                                              srcs=[src], dsts=[dst] * len(cores))], local_sem=T.sem.sent)
        total["sent"] = total.get("sent", 0) + len(eng)

    def spread(src, slot, rd, key):
        order("g", rd, [], ())
        s, v = "arr%d" % count["arr"], "via%d" % count["arr"]
        count["arr"] += 1
        send([partner], v, src, slot(r))
        send(near, s, src, slot(r))
        total[v] = len(eng)
        wait("g", (v, total[v]))
        theirs = slot(T.rank_of(partner))
        send(near, s, theirs, theirs)
        total[s] = 2 * len(eng) * len(near)
        wrote[key] = (s, total[s])
        wrote[key + "v"] = (v, total[v])

    V, S, P = g.vector, g.scalar, g.tensor

    def ts(out, in0, s1, s2, o0, o1, rd, wr, banks=()):
        if o1 is None:
            op("v", lambda: V.tensor_scalar(out, in0, s1, None, o0), rd, wr, banks)
        else:
            op("v", lambda: V.tensor_scalar(out, in0, s1, s2, o0, o1), rd, wr, banks)

    def tt(out, in0, in1, o, rd, wr, banks=()):
        op("v", lambda: V.tensor_tensor(out, in0, in1, o), rd, wr, banks)

    def cp(out, in_, rd, wr, banks=()):
        op("v", lambda: V.tensor_copy(out, in_), rd, wr, banks)

    def fill(out, value, wr):
        op("v", lambda: V.memset(out, value), [], wr)

    def act(out, in_, f, bias, scale, rd, wr, banks=()):
        op("a", lambda: S.activation(out, in_, f, bias=bias, scale=scale), rd, wr, banks)

    def mm(out, lhsT, rhs, start, stop, rd, wr, banks, inc=True):
        op("t", lambda: P.matmul(out, lhsT, rhs, start, stop), rd, wr, banks, inc)

    def names(k, i0, i1):
        return ["%s@%d" % (k, b) for b in range(i0 // 8, (i1 + 7) // 8)]

    def full(k):
        return names(k, 0, L)

    def pairs(cuts):
        return list(zip(cuts, cuts[1:]))

    def slots(buf, c0):
        return lambda q: buf[:, c0 + L * q:c0 + L * (q + 1)]

    mp, sl, rr, more = T.p1[:, L:2 * L], T.p4[:, 0:32], T.p6[0:8, L:2 * L], T.p5[:, 0:L]
    step, shift, cc, bb, u1 = T.p6[:, 0:L], T.p7[:, L:2 * L], T.p7[:, 0:L], T.bu[:, 0:L], T.bu[:, L:2 * L]
    thc, bc, jc, j5 = T.cols[:, 0:1], T.cols[:, 1:2], T.cols[:, 2:3], T.cols[:, 3:4]

    def make_cc(t):
        act(cc, T.m2[:], F.Relu, K - M * (t + 1) - BIG, 1.0, ["m2"], ["cc"], [7])

    dma("a", T.omi[:], T.om[:], [], ["om"])
    dma("s", T.coli[:], T.col[:], [], ["col"])
    dma("s", T.mti[:, 0:L], T.mem[:], [], ["mem"])
    dma("a", T.mti[:, L:L + 1], T.th[:], [], ["th"])
    fill(T.ones[:], 1.0, ["ones"])
    op("g", lambda: g.iota(T.pi[:, 0:1], [[0, 1]], 0, 1), [], ["pi"])
    op("g", lambda: g.iota(T.ua[:], [[77, 3], [80, 16]], L * r + 77, 0, allow_small_or_imprecise_dtypes=True), [], ["base"])
    op("g", lambda: g.affine_select(T.e1[:], T.ones[0:8, 0:128], [[1, 128]], A.is_ge, 0.0, 0, -16), ["ones"], ["e1"])
    op("g", lambda: g.affine_select(T.ey[:, 128:272], T.ones[0:8, 0:144], [[1, 144]], A.is_equal, 0.0, -15, -16), ["ones"], ["ey1"])
    op("g", lambda: g.affine_select(T.ey[:, 0:128], T.e1[:], [[-1, 128]], A.is_ge, 0.0, 15, 16), ["e1"], ["ey0"])
    fill(u1, C + K, full("u1"))
    ts(T.pi[:, 4:5], T.pi[:, 0:1], 15, None, A.bitwise_and, None, ["pi"], ["pj"])
    fill(T.base[:], 0.0, ["bs"])
    ts(j5, T.pi[:, 4:5], 5.0, None, A.mult, None, ["pj"], ["j5"])
    cp(jc, T.pi[:, 4:5], ["pj"], ["jc"])
    ts(T.cols[:, 4:5], T.pi[:, 4:5], 5.0, 8 * 61 - 16 * (C / K + 1), A.mult, A.add, ["pj"], ["c4"])
    ts(T.ui[:, 0:16], T.ua[:, 0:16], j5, -77.0, A.add, A.add, ["base", "j5"], ["u4"])
    for t in range(RO - 1):
        ts(T.base[:, 32 * t + 16:32 * t + 32], T.ua[:, 16 * t:16 * t + 16], T.cols[:, 4:5], K, A.add, A.mult,
           ["base", "c4", "bs"], ["bs%d" % t])
    ts(T.ui[:, 16:32], T.ui[:, 0:16], M - 1, None, A.bitwise_and, None, ["u4"], ["u5"])
    mine = slots(T.tab, 0)(r)
    ts(mp, T.omi[:], 1.0 / 8192, None, A.mult, None, ["om"], full("mp"), [1])
    cp(T.ol[:, 0:16], T.ui[:, 16:32], ["u5"], ["ol"])
    tt(mine, T.coli[:], mp, A.add, ["col"] + full("mp"), ["own0"], [1])
    op("g", lambda: g.iota(T.lev[:], [[1, L]], int(BIG) + L * r, 0, allow_small_or_imprecise_dtypes=True), [], ["lev"])
    spread(mine, slots(T.tab, 0), ["own0"], "far0")

    op("g", lambda: g.affine_select(T.eye[:], T.ones[:, 0:128], [[-1, 128]], A.is_equal, 0.0, 0, 1), ["ones"], ["eye"])
    cp(T.mtb[:, 0:L + 1], T.mti[:, 0:L + 1], ["mem", "th"], ["mtb"])
    mm(T.p2[:, 0:272], T.ey[:, 0:128], T.ey[:], True, True, ["ey0", "ey1"], ["blk"], [2])
    mm(T.p3[:, 0:L + 1], T.ey[:, 0:128], T.mtb[:, 0:L + 1], True, True, ["ey0", "mtb"], ["mt"], [3])
    act(T.m1[:], T.lev[:], F.Identity, 0.0, 1.0 / M, ["lev"], ["m1"])
    act(T.m2[:], T.lev[:], F.Identity, 2 * BIG / M, -1.0 / M, ["lev"], ["m2"])
    act(T.bo[:, 0:128], T.p2[:, 0:128], F.Copy, 0.0, FAR, ["blk"], ["bo"], [2])
    act(T.zs[:], T.p2[:, 128:272], F.Copy, 0.0, 1.0, ["blk"], ["zs"], [2])
    for n, wgt in enumerate([1.0 / (16 * K), 1.0 / 32]):
        act(T.et[:, 8 * n:8 * n + 8], T.p2[:, 0:128:16], F.Copy, 0.0, wgt, ["blk"], ["et%d" % n], [2])
    ts(T.zi[:], T.omi[:], -1.0, None, A.mult, None, ["om"], ["zi"])
    ts(step, T.p3[:, 0:L], jc, float(M), A.is_equal, A.mult, ["mt", "jc"], ["step"], [3, 6])
    ts(T.qi[:], T.zi[:], 4095, None, A.bitwise_and, None, ["zi"], full("qi"))
    tt(T.m1[:], T.m1[:], step, A.mult, ["m1", "step"], ["m1"], [6])
    cp(thc, T.p3[:, L:L + 1], ["mt"], ["thc"], [3])
    act(cc, T.m1[:], F.Relu, M - L * r - BIG, 1.0, ["m1"], ["cc"], [7])
    cp(mp, T.qi[:], full("qi"), full("mp"), [1])
    tt(T.m2[:], T.m2[:], step, A.mult, ["m2", "step"], ["m2"], [6])
    ts(shift, T.p3[:, 0:L], jc, float(L * r), A.is_equal, A.mult, ["mt", "jc"], ["shift"], [3, 7])
    ts(T.cols[:, 5:6], thc, -2 * FAR, 17 * FAR, A.mult, A.add, ["thc"], ["c5"])
    ts(bc, thc, 2.0, -16.0, A.mult, A.add, ["thc"], ["bc"])
    ts(T.cols[:, 6:7], thc, -2.0, 17.0, A.mult, A.add, ["thc"], ["c6"])
    ts(T.cols[:, 7:8], thc, -1.0, 0.5, A.mult, A.add, ["thc"], ["c7"])
    tt(T.ys[:], mine, cc, A.max, ["own0", "cc"], ["ys"], [7])
    act(T.one[:], step, F.Copy, 0.0, 1.0, ["step"], ["one"], [6])
    act(T.lim[:, 0:L], T.ones[:], F.Identity, 0.0, T.cols[:, 5:6], ["ones", "c5"], ["lim"])
    make_cc(0)
    act(T.bo[:, 128:256], T.bo[:, 0:128], F.Copy, 0.0, -1.0, ["bo"], ["nbo"])
    act(T.lim[:, L:2 * L], T.lim[:, 0:L], F.Copy, 0.0, -1.0, ["lim"], ["nlim"])
    act(T.eyef[:, 0:128], T.eye[:], F.Copy, 0.0, 1.0, ["eye"], ["eyef"])
    act(T.eyef[:, 128:256], T.eye[:], F.Copy, 0.0, -1.0, ["eye"], ["negf"])

    for t in range(RO):
        last = t == RO - 1
        e0 = M * (t + 1)
        par = T.tab[:, M * t:e0]
        tabs = ["own%d" % s for s in range(t + 1)] + ["far%d" % s for s in range(t + 1)] + ["zero%d" % s for s in range(1, t + 1)]
        heads = pairs(HEADS)
        y, fs = T.tab[:, e0:e0 + L], ["y%d_%d" % (t, h) for h in range(len(heads))]

        def vector(h):
            i0, i1 = heads[h]
            tt(T.tab[:, e0 + i0:e0 + i1], par.indirect(T.ol[:, i0 // 16:i1 // 16]), T.ys[:, i0:i1], A.max,
               tabs[t::t + 1][:2] + tabs[-1:] + ["ol", "ys"], [fs[h]])

        def offsets(h):
            i0, i1 = heads[h]
            cp(T.off[:, i0:i1], T.tab[:, e0 + i0:e0 + i1], [fs[h]], ["off%d" % h])
            for c0, c1 in pairs(GATHER[t]):
                if i0 <= c0 < i1:
                    act(T.gat[:, 16 * c0:16 * c1], T.tab[:, 0:e0 + i1].indirect(T.off[:, c0:c1]), F.Copy, 0.0, 1.0,
                        tabs + fs[:h + 1] + ["off%d" % h], names("ga", c0, c1))

        vector(0)
        for h in range(1, len(heads)):
            vector(h)
            offsets(h - 1)
        if t == 0:
            ts(T.zi[:], par.indirect(T.ol[:, 0:16]), -8192.0, None, A.mult, None, ["own0", "far0", "ol"], ["zi"])
        offsets(len(heads) - 1)
        if t == 0:
            ts(T.qi[:], T.zi[:], 4095, None, A.bitwise_and, None, ["zi"], full("qi"))

        def slot(q):
            return slots(T.zero, L * t)(0) if q == 0 else slots(T.tab, e0)(q)

        def share(n):
            if n < len(SHARE[t]) - 1:
                c0, c1 = SHARE[t][n:n + 2]
                cp(T.gat[:, 16 * c0:16 * c1], T.tab[:, 0:e0 + L].indirect(T.off[:, c0:c1]), tabs + fs + ["off%d" % (len(heads) - 1)],
                   names("ga", c0, c1))

        def onward():
            if not last:
                mm(more, T.eyef[:, 0:128], y, True, False, fs + ["eyef"], ["more"], [5], False)
                mm(more, T.eye[:], T.one[:], False, True, ["eye", "one"], ["more"], [5])

        def vectors():
            if last:
                tt(T.ox[:], y, shift, A.add, fs + ["shift"], ["ox"], [7])
            elif r == 0:
                spread(y, slot, fs, "far%d" % (t + 1))
            else:
                tt(slot(r), y, shift, A.add, fs + ["shift"], ["own%d" % (t + 1)], [7])
                spread(slot(r), slot, ["own%d" % (t + 1)], "far%d" % (t + 1))

        if t > 0:
            vectors()
        top = COMPARE[t][-1]
        parts = [(0, HALF, 3, T.p3, 4, T.p4), (HALF, L, 2, T.p2, 7, T.p7)]
        for i0, i1, b, pb, d, pd in parts:
            mm(pb[:, i0:i1], T.eye[:], T.lim[:, i0:i1], True, False, ["eye", "lim"], names("sj", i0, i1), [b], False)
            if last:
                mm(pd[:, i0:i1], T.eye[:], T.lim[:, L + i0:L + i1], True, False, ["eye", "nlim"], names("nj", i0, i1), [d], False)
        if not last:
            mm(sl, T.eyef[:, 0:128], T.base[:, 32 * t:32 * t + 32], True, False, ["eyef", "bs%d" % t], ["sl"], [4], False)
        marks = [(0, HALF, 0, T.p0), (HALF, L, 6, T.p6)]
        counts = [(1, T.p1), (0, T.p0)]

        def level(n):
            act(T.orr[:, L * n:L * n + L], rr, F.Identity, -0.5 - C / K, 1.0, ["rr"], ["orr%d" % n], [6])

        def lanes():
            ts(T.nl[:, top:L], T.p6[:, top:L], -1.0, 0.5, A.mult, A.add, names("lo", top, L), ["nl"], [6])
            for i in range(top, L):
                op("a", lambda: S.activation(T.signs[:, 16 * (i - top):16 * (i - top + 1)], T.gat[:, 16 * i:16 * i + 16], F.Sign,
                                             bias=T.nl[:, i:i + 1], scale=1.0, accum_out=T.cs[:, i:i + 1]),
                   names("ga", top, L) + ["nl"], ["cs"] if i == L - 1 else [], (), i == L - 1)

        if t == 0:
            share(0)
            tt(T.tmp[:], T.qi[:], mp, A.max, full("qi") + full("mp"), ["tmp"], [1])
            share(1)
            for i0, i1, b, pb in marks:
                ts(pb[:, i0:i1], T.tmp[:, i0:i1], -1.0, 4096.0, A.mult, A.add, ["tmp"], names("lo", i0, i1), [b])
            vectors()
            onward()
            act(T.key[:], T.tmp[:], F.Identity, C, 1.0, ["tmp"], full("key"))
        else:
            onward()
            share(0)
            if last:
                mm(more, T.eye[:], T.lim[:, 0:L], True, False, ["eye", "lim"], ["more"], [5], False)
                ts(T.ox[:], T.ox[:], WHOLE, -WHOLE, A.add, A.add, ["ox"], ["ox"])
            for i0, i1, b, pb in marks:
                tt(T.key[:, i0:i1], T.ft[:, M * (t - 1):M * t].indirect(T.ol[:, i0 // 16:i1 // 16]), T.ks[:, i0:i1], A.max,
                   ["fown%d_0" % (t - 1), "fown%d_1" % (t - 1), "ffar%d" % (t - 1), "ks", "ol"], names("key", i0, i1))
            for i0, i1, b, pb in marks:
                mm(pb[:, i0:i1], T.eyef[:, 128:256], T.key[:, i0:i1], True, False, names("key", i0, i1) + ["negf"],
                   names("lo", i0, i1), [b], False)
                ts(T.bu[:, L + i0:L + i1], T.key[:, i0:i1], K / 2 + 0.5, None, A.add, None, names("key", i0, i1), names("u1", i0, i1))
                mm(pb[:, i0:i1], T.eye[:], T.bu[:, L + i0:L + i1], False, True, names("u1", i0, i1) + ["eye"], names("lo", i0, i1), [b])

            share(1)
            if last:
                dma("s", T.yx[:], T.ox[:], ["ox"] + full("key"), [])
                dma("s", T.yr[:, 0:L * t], T.orr[:, 0:L * t], ["orr%d" % n for n in range(t)], [])

        def known(i0, i1, b, pb):
            ts(T.tmp[:, i0:i1], pb[:, i0:i1], K, None, A.is_lt, None, names("lo", i0, i1), names("tm", i0, i1), [b])

        def kept(i0, i1, b, pb):
            tt(T.kn[:, i0:i1], T.tmp[:, i0:i1], pb[:, i0:i1], A.mult, names("tm", i0, i1) + names("lo", i0, i1), names("kn", i0, i1), [b])

        def settle():
            if r > 0:
                act(y, slot(0), F.Copy, 0.0, 1.0, ["far%d" % (t + 1)], fs + ["zero%d" % (t + 1)])
            else:
                wrote["own%d" % (t + 1)] = wrote[fs[-1]]

        def reach(i0, i1, b, pb, d, pd):
            c1, (e, pe) = min(i1, top), counts[i0 >= HALF]
            act(T.bu[:, i0:c1], pe[:, i0:c1], F.Sign, T.cols[:, 7:8], 1.0, names("cnt", i0, c1) + ["c7"], names("bb", i0, c1), [e])
            mm(pb[:, i0:i1], T.bo[:, 0:128], T.bu[:, i0:i1], False, True, names("bb", i0, i1) + ["bo"], names("sj", i0, i1), [b])
            if last:
                mm(pd[:, i0:i1], T.bo[:, 128:256], T.bu[:, i0:i1], False, True, names("bb", i0, i1) + ["nbo"], names("nj", i0, i1), [d])

        for n, (c0, c1) in enumerate(pairs(COMPARE[t])):
            if n > 0 and t == 0:
                share(n + 1)
            b, pb = marks[c0 >= HALF][2:]
            for k in range(16):
                if top < L and (n, k) == (0, 3):
                    lanes()
                ck = ["cmp%d_%d" % (k, c0)]
                tt(T.cmp[:, L * k + c0:L * k + c1], T.gat[:, 16 * c0 + k:16 * c1:16], pb[:, c0:c1], A.is_ge,
                   names("ga", c0, c1) + names("lo", c0, c1), ck, [b])
                mm(counts[c0 >= HALF][1][:, c0:c1], T.eye[:], T.cmp[:, L * k + c0:L * k + c1], k == 0, k == 15,
                   ck + ["eye"], names("cnt", c0, c1), [counts[c0 >= HALF][0]], k == 15)
                if last and (c1, k) == (HALF, 12):
                    known(*marks[0])
                if last and (c1, k) == (HALF, 14):
                    kept(*marks[0])
        if t == 0:
            ts(T.p6[:, L:2 * L], T.tmp[:], 0.0, K - 4096, A.is_gt, A.mult, ["tmp"], ["has"], [6])
        if not last:
            tt(T.kn[:], u1, cc, A.add, full("u1") + ["cc"], full("kn"), [7])
        if t == 0:
            tt(T.key[:], T.p6[:, L:2 * L], T.key[:], A.add, ["has"] + full("key"), full("key"), [6])
        if last:
            known(*marks[1])
            kept(*marks[1])
        reach(*parts[0])
        if top < L:
            act(T.bu[:, top:L], T.cs[:, top:L], F.Sign, T.cols[:, 6:7], 1.0, ["cs", "c6"], names("bb", top, L))
        reach(*parts[1])
        if last:
            mm(more, T.bo[:, 0:128], bb, False, True, full("bb") + ["bo"], ["more"], [5])
            mm(rr, T.et[:, 0:8], u1, True, False, ["et0"] + full("u1"), ["rr"], [6], False)
            act(T.sb[:], more, F.Sign, 0.0, 1.0, ["more"], full("sb"), [5])
            mm(rr, T.et[:, 8:16], T.sb[:], False, True, ["et1"] + full("sb"), ["rr"], [6])
            level(t)
            dma("a", T.yr[:, L * t:L * t + L], T.orr[:, L * t:L * t + L], ["orr%d" % t], [])
            for i0, i1, b, pb, d, pd in parts:
                tt(T.p1[:, L + i0:L + i1], pb[:, i0:i1], T.lev[:, i0:i1], A.min, names("sj", i0, i1) + ["lev"], names("mp", i0, i1), [1, b])
                tt(T.tmp[:, i0:i1], pd[:, i0:i1], T.kn[:, i0:i1], A.min, names("nj", i0, i1) + names("kn", i0, i1), names("tm", i0, i1), [d])
            for i0, i1, b, pb, d, pd in parts:
                tt(T.oo[:, i0:i1], T.p1[:, L + i0:L + i1], T.tmp[:, i0:i1], A.max, names("mp", i0, i1) + names("tm", i0, i1),
                   names("oo", i0, i1), [1])
            dma("s", T.yo[:], T.oo[:], full("oo"), [])
            break
        for p in range(16):
            mm(sl, T.zs[:, 15 - p:143 - p], T.bu[:, p:2 * L:16], False, p == 15, full("bb") + full("u1") + ["zs"], ["sl"], [4],
               p == 15)
        fown, fn = slots(T.ft, M * t)(r), ["fown%d_0" % t, "fown%d_1" % t]
        for n, (i0, i1, b, pb, d, pd) in enumerate(parts):
            tt(T.p1[:, L + i0:L + i1], pb[:, i0:i1], T.kn[:, i0:i1], A.min, names("sj", i0, i1) + names("kn", i0, i1),
               names("mp", i0, i1), [1, b])
        for n, (i0, i1, b, pb, d, pd) in enumerate(parts):
            tt(T.ft[:, M * t + L * r + i0:M * t + L * r + i1], T.p1[:, L + i0:L + i1], T.key[:, i0:i1], A.max,
               names("mp", i0, i1) + names("key", i0, i1), [fn[n]], [1])
            act(T.sb[:, i0:i1], pb[:, i0:i1], F.Sign, 0.0, 1.0, names("sj", i0, i1), names("sb", i0, i1), [b])
        spread(fown, slots(T.ft, M * t), fn, "ffar%d" % t)
        act(T.ks[:], fown, F.Copy, 0.0, 1.0, fn, ["ks"])
        act(T.ys[:], more, F.Copy, 0.0, 1.0, ["more"], ["ys"], [5])
        settle()
        if t + 2 < RO:
            make_cc(t + 1)
        else:
            act(T.lev[:], T.m1[:], F.Relu, M * RO - BIG, 1.0, ["m1"], ["lev"])
        ts(T.ua[:, 0:16], T.p4[:, 0:16], bc, 16 * K, A.is_ge, A.mult, ["sl", "bc"] + ["bs%d" % n for n in range(3)], ["u1a"], [4])
        ts(T.ua[:, 16:32], T.p4[:, 0:16], 30.5 * K, None, A.mult, None, ["sl"], ["u1b"], [4])
        tt(T.ua[:, 32:48], T.p4[:, 16:32], T.ua[:, 0:16], A.add, ["sl", "u1a"], ["u2"], [4])
        tt(T.ui[:, 0:16], T.ua[:, 32:48], T.ua[:, 16:32], A.add, ["u1b", "u2"], ["u4"])
        ts(T.ui[:, 16:32], T.ui[:, 0:16], 14, M - 1, A.arith_shift_right, A.bitwise_and, ["u4"], ["u5"])
        cp(T.ol[:, 0:16], T.ui[:, 16:32], ["u5"], ["ol"])
        mm(rr, T.et[:, 0:8], u1, True, False, ["et0"] + full("u1"), ["rr"], [6], False)
        mm(rr, T.et[:, 8:16], T.sb[:], False, True, ["et1"] + full("sb"), ["rr"], [6])
        level(t)
    for s in total:
        wait("g", (s, total[s]))
